import numpy as np
import ml_dtypes


def mxq(x, axis, fmt="e4m3"):
    dtype, down = {"e4m3": (ml_dtypes.float8_e4m3fn, 7), "e5m2": (ml_dtypes.float8_e5m2, 14)}[fmt]
    v = np.moveaxis(np.asarray(x, np.float32).astype(ml_dtypes.bfloat16).astype(np.float64), axis, -1)
    blocks = v.reshape(v.shape[:-1] + (-1, 32))
    amax = np.abs(blocks).max(-1, keepdims=True)
    byte = np.maximum(np.where(amax > 0, np.frexp(amax)[1] - 1 + 127, 0) - down, 1)
    scale = np.exp2(byte - 127.0)
    codes = (blocks / scale).astype(np.float32).astype(dtype).astype(np.float64)
    return np.moveaxis((codes * scale).reshape(v.shape), -1, axis)


WIDE = False


def mx_kscale(k):
    if not WIDE:
        return np.ones(k)
    levels = np.array([10, -10, 5, -5, 0])
    if k % 512:
        return np.exp2(np.random.permutation(np.resize(levels, k // 32))).repeat(32)
    a = np.empty((k // 512, 16))
    for p in range(k // 512):
        a[p, :8] = np.random.permutation(np.resize(levels, 8))
        for g in range(8):
            far = levels[np.abs(levels - a[p, g]) >= 10]
            a[p, g + 8] = far[np.random.randint(len(far))]
    return np.exp2(a.ravel()).repeat(32)


def f64(x):
    return np.asarray(x).astype(np.float64)


def striped(idx):
    return np.tile(idx.reshape(-1, 16).T, (8, 1)).astype(np.uint16)


def unstriped(offs):
    return offs[:16].T.reshape(-1).astype(np.int64)


E2M1 = np.array([0.0, 0.5, 1.0, 1.5, 2.0, 3.0, 4.0, 6.0, -0.0, -0.5, -1.0, -1.5, -2.0, -3.0, -4.0, -6.0])


def pack_weight(w, fmt):
    k, n = w.shape
    w = f64(np.asarray(w, np.float32).astype(ml_dtypes.bfloat16)).reshape(k // 32, 32, n)
    amax = np.abs(w).max(1)
    if fmt == "e4m3":
        byte = np.frexp(amax)[1] - 1 + 127 - 7
    else:
        mant, ex = np.frexp(amax / 6.0)
        byte = np.where(mant > 0.5, ex, ex - 1) + 127
    byte = np.clip(np.where(amax > 0, byte, 1), 1, 254)
    scaled = (w * np.exp2(127.0 - byte)[:, None, :]).reshape(k, n).astype(np.float32)
    by_word = np.ascontiguousarray(scaled.reshape(k // 512, 128, 4, n).transpose(0, 1, 3, 2))
    if fmt == "e4m3":
        words = by_word.astype(ml_dtypes.float8_e4m3fn).view(np.uint8)
    else:
        c = by_word.astype(ml_dtypes.float4_e2m1fn).view(np.uint8) & 0xF
        words = (c[..., 0::2] | (c[..., 1::2] << 4)).reshape(k // 512, 128, 2 * n)
    return np.ascontiguousarray(words), np.ascontiguousarray(byte.astype(np.uint8).reshape(k // 512, 16, n))


def unpack_weight(words, scales, fmt):
    g, _, n = scales.shape
    words = np.ascontiguousarray(words).reshape(g, 128, n, -1)
    if fmt == "e4m3":
        vals = words.view(ml_dtypes.float8_e4m3fn).astype(np.float64)
    else:
        nib = np.empty((g, 128, n, 4), np.uint8)
        nib[..., 0::2] = words & 0xF
        nib[..., 1::2] = words >> 4
        vals = E2M1[nib]
    vals = vals * np.repeat(np.exp2(scales.astype(np.float64) - 127.0), 8, axis=1)[..., None]
    return vals.transpose(0, 1, 3, 2).reshape(g * 512, n)


def gelu(v):
    return 0.5 * v * (1.0 + np.tanh(np.sqrt(2.0 / np.pi) * (v + 0.044715 * v**3)))


def often(T, S):
    return np.random.permutation(T)[(T * np.random.uniform(0, 1, S) ** 4).astype(np.int64)]


def bf(x):
    return np.asarray(x, np.float32).astype(ml_dtypes.bfloat16)


def planes(Y):
    n, m = Y.shape
    b = f64(bf(Y)).reshape(n // 32, 32, m)
    amax = np.abs(b).max(1)
    byte = np.clip(np.where(amax > 0, np.frexp(amax)[1] - 1 + 127 - 7, 1), 1, 254)
    codes = (b * np.exp2(127.0 - byte)[:, None, :]).reshape(n, m).astype(np.float32).astype(ml_dtypes.float8_e4m3fn).view(np.uint8)
    words = codes.reshape(n // 512, 128, 4, m).transpose(0, 1, 3, 2)
    return np.ascontiguousarray(words), np.ascontiguousarray(byte.astype(np.uint8).reshape(n // 512, 16, m))


K, K2, K3, H, N, T, S, P = 1024, 512, 512, 1024, 512, 2048, 1024, 512

def setup_inputs():
    n = np.random.standard_normal
    s, s2, s3 = mx_kscale(K)[:, None], mx_kscale(K2)[:, None], mx_kscale(K3)[:, None]
    u = mx_kscale(H)[:, None]
    spread = np.exp(0.8 * n(N))[None, :]
    d = {}
    d["tab_words"], d["tab_scales"] = pack_weight(n((K, T)) * s, "e4m3")
    d["tab2_words"], d["tab2_scales"] = pack_weight(n((K2, T)) * s2, "e4m3")
    d["tab3_words"], d["tab3_scales"] = pack_weight(n((K3, T)) * s3, "e4m3")
    d["offs"] = striped(np.random.permutation(T)[:S])
    d["offs2"] = striped(np.random.permutation(T)[:S])
    d["offs3"] = striped(np.random.permutation(T)[:S])
    d["pos1"] = striped(np.random.permutation(S)[:P])
    d["pos2"] = striped(often(S, P))
    d["pos3"] = striped(often(S, P))
    d["w1"] = (0.55 * n((K, H)) / K ** 0.5 / s).astype(np.float32)
    d["w2_words"], d["w2_scales"] = pack_weight(n((K2, H)) / K2 ** 0.5 / s2, "e2m1")
    d["w3_words"], d["w3_scales"] = pack_weight(0.55 * n((K3, H)) / K3 ** 0.5 / s3, "e4m3")
    d["gain"] = (np.exp(0.3 * n(H)) * u[:, 0]).astype(np.float32)
    d["w4_words"], d["w4_scales"] = pack_weight(n((H, N)) / H ** 0.5 / u * spread, "e2m1")
    d["w5"] = (n((H, N)) / H ** 0.5 / u * spread).astype(np.float32)
    return d

def reference(tab_words, tab_scales, tab2_words, tab2_scales, tab3_words, tab3_scales, offs, offs2, offs3, pos1, pos2, pos3, w1, w2_words, w2_scales, w3_words, w3_scales, gain, w4_words, w4_scales, w5):
    v = unpack_weight(tab_words, tab_scales, "e4m3")[:, unstriped(offs)]
    v2 = unpack_weight(tab2_words, tab2_scales, "e4m3")[:, unstriped(offs2)]
    v3 = unpack_weight(tab3_words, tab3_scales, "e4m3")[:, unstriped(offs3)]
    a = mxq(f64(w1), 0, "e4m3").T @ v
    b = unpack_weight(w2_words, w2_scales, "e2m1").T @ v2
    d = unpack_weight(w3_words, w3_scales, "e4m3").T @ v3
    ap = a[:, unstriped(pos1)]
    bp = b[:, unstriped(pos2)]
    dp = d[:, unstriped(pos3)]
    z = f64(gain)[:, None] * (np.sin(ap) * bp + np.cos(dp) * ap)
    w4 = unpack_weight(w4_words, w4_scales, "e2m1")
    y = w4.T @ mxq(z, 0, "e4m3") + mxq(f64(w5), 0, "e4m3").T @ mxq(np.abs(z), 0, "e4m3")
    words, scales = planes(y)
    return y, words, scales

@@ -1,0 +1,302 @@
+import math
+from contextlib import ExitStack
+
+import concourse.mybir as mybir
+
+K, K2, K3, H, N, T, S, PJ = 1024, 512, 512, 1024, 512, 2048, 1024, 512
+FLOPS = 2 * H * S * (K + K2 + K3) + 2 * 2 * H * N * PJ
+
+F32 = mybir.dt.float32
+BF16 = mybir.dt.bfloat16
+I32 = mybir.dt.int32
+U32 = mybir.dt.uint32
+U16 = mybir.dt.uint16
+U8 = mybir.dt.uint8
+FP8X4 = mybir.dt.float8_e4m3fn_x4
+FP4X4 = mybir.dt.float4_e2m1fn_x4
+ALU = mybir.AluOpType
+ACT = mybir.ActivationFunctionType
+
+P = 128
+BANK = 512
+SLICES = H // P
+TWO_PI = 2.0 * math.pi
+JB = 128
+
+
+def tile_list_holding_stack_features_kernel(
+    tc, tab_words, tab_scales, tab2_words, tab2_scales, tab3_words, tab3_scales,
+    offs, offs2, offs3, pos1, pos2, pos3, w1, w2_words, w2_scales, w3_words, w3_scales,
+    gain, w4_words, w4_scales, w5, out_0, out_1, out_2,
+):
+    nc = tc.nc
+    with ExitStack() as ctx:
+        lists = ctx.enter_context(tc.tile_pool(name="lists", bufs=1))
+        keep = ctx.enter_context(tc.tile_pool(name="keep", bufs=1))
+        ring = ctx.enter_context(tc.tile_pool(name="ring", bufs=2))
+        psum = ctx.enter_context(tc.psum_pool(name="psum", bufs=1))
+
+        def big(shape, dtype, name):
+            return ring.tile(shape, dtype, name=name, tag="big", bufs=7, align_bytes=64)
+
+        def load_list(src, name):
+            t = lists.tile(list(src.shape), U16, name=name)
+            nc.sync.dma_start(t[:], src)
+            return t
+
+        def load_table_words(words, a, name):
+            t = big([P, T], I32, name)
+            nc.sync.dma_start(t[:], words[a].rearrange("p t i -> p (t i)").bitcast(I32))
+            return t
+
+        def load_weight_rows(w, a, c0, name):
+            t = big([P, 4, BANK], F32, name)
+            nc.sync.dma_start(t[:], w[512 * a : 512 * (a + 1), c0 : c0 + BANK].rearrange("(p j) c -> p j c", j=4))
+            return t
+
+        def zeroed_plane(width, name):
+            t = keep.tile([P, width], U8, name=name, align_bytes=64)
+            nc.vector.memset(t[:].bitcast(I32), 0)
+            return t
+
+        def load_scale_rows(queue, plane, scales, first_row):
+            rows = 4 * scales.shape[0]
+            for q in range(4):
+                p0 = 32 * q + first_row
+                queue.dma_start(plane[p0 : p0 + rows, :].bitcast(I32), scales[:, 4 * q : 4 * q + 4, :].bitcast(I32))
+
+        ts1 = zeroed_plane(T, "ts1")
+        ts2 = zeroed_plane(T, "ts2")
+        ts3 = zeroed_plane(T, "ts3")
+        ws23 = zeroed_plane(H, "ws23")
+        ws4 = zeroed_plane(2 * N, "ws4")
+        load_scale_rows(nc.scalar, ts1, tab_scales, 0)
+        load_scale_rows(nc.scalar, ts2, tab2_scales, 0)
+        load_scale_rows(nc.scalar, ts3, tab3_scales, 0)
+        load_scale_rows(nc.gpsimd, ws23, w2_scales, 0)
+        load_scale_rows(nc.gpsimd, ws23, w3_scales, 4)
+        for q in range(4):
+            nc.gpsimd.dma_start(
+                ws4[32 * q : 32 * q + 4, :].bitcast(I32).rearrange("p (a c) -> p a c", a=2),
+                w4_scales[:, 4 * q : 4 * q + 4, :].bitcast(I32).rearrange("a r c -> r a c"),
+            )
+
+        l_offs = load_list(offs, "l_offs")
+        tw10 = load_table_words(tab_words, 0, "tw10")
+        tw11 = load_table_words(tab_words, 1, "tw11")
+        w1_raw = {}
+        for a in range(2):
+            w1_raw[a, 0] = load_weight_rows(w1, a, 0, f"w1r{a}0")
+        l_offs2 = load_list(offs2, "l_offs2")
+        tw2 = load_table_words(tab2_words, 0, "tw2")
+        w2_raw = keep.tile([P, 2 * H], U8, name="w2_raw")
+        nc.sync.dma_start(w2_raw[:].bitcast(I32), w2_words[0].bitcast(I32))
+        l_offs3 = load_list(offs3, "l_offs3")
+        tw3 = load_table_words(tab3_words, 0, "tw3")
+        w3_raw = keep.tile([P, H], I32, name="w3_raw")
+        nc.sync.dma_start(w3_raw[:], w3_words[0].rearrange("p c i -> p (c i)").bitcast(I32))
+        l_pos1 = load_list(pos1, "l_pos1")
+        l_pos3 = load_list(pos3, "l_pos3")
+        l_pos2 = load_list(pos2, "l_pos2")
+        gain_sb = keep.tile([P, SLICES], F32, name="gain_sb")
+        nc.sync.dma_start(gain_sb[:].rearrange("p (g t) -> p g t", t=4), gain.rearrange("(g p t) -> p g t", p=P, t=4))
+        for a in range(2):
+            w1_raw[a, 1] = load_weight_rows(w1, a, BANK, f"w1r{a}1")
+        w4_raw = keep.tile([P, 2, 2 * N], U8, name="w4_raw")
+        nc.sync.dma_start(w4_raw[:].bitcast(I32), w4_words.bitcast(I32).rearrange("a p c -> p a c"))
+        w5_raw = [load_weight_rows(w5, g, 0, f"w5r{g}") for g in range(2)]
+
+        def gather_words(table, offsets, name):
+            t = keep.tile([P, S], U32, name=name, align_bytes=64)
+            nc.vector.tensor_copy(t[:], table[:].bitcast(U32).indirect(offsets[:]))
+            return t
+
+        def gather_scales(plane, offsets, name):
+            t = keep.tile([P, S], U8, name=name, align_bytes=64)
+            nc.vector.tensor_copy(t[:], plane[:].indirect(offsets[:]))
+            return t
+
+        def deal(dst, src, run):
+            nc.vector.tensor_copy(
+                dst.rearrange("p (g t c i) -> p g c t i", g=2, t=4, i=run),
+                src.rearrange("p (g c i t) -> p g c t i", g=2, t=4, i=run),
+            )
+
+        def round_weight(raw, name):
+            wb = ring.tile([P, 4 * BANK], BF16, name=name, tag="wb", align_bytes=64)
+            nc.scalar.copy(
+                wb[:].rearrange("p (t q j) -> p q j t", t=4, j=4),
+                raw[:].rearrange("p j (q t) -> p q j t", t=4),
+            )
+            return wb
+
+        def quantize(src, width, name, pool=keep, tag=None, bufs=None):
+            kw = {} if tag is None else {"bufs": bufs}
+            codes = pool.tile([P, width], U32, name=name + "_c", tag=(tag or name) + "_c", align_bytes=64, **kw)
+            scales = pool.tile([P, width], U8, name=name + "_s", tag=(tag or name) + "_s", align_bytes=64, **kw)
+            nc.vector.quantize_mx(out=codes[:].bitcast(FP8X4), scales=scales[:], in_=src)
+            return codes, scales
+
+        v10 = gather_words(tw10, l_offs, "v10")
+        v11 = gather_words(tw11, l_offs, "v11")
+        vs1 = gather_scales(ts1, l_offs, "vs1")
+        w1_q = {}
+        for a in range(2):
+            w1_q[a, 0] = quantize(round_weight(w1_raw[a, 0], f"w1b{a}0")[:], BANK, f"w1q{a}0")
+        v2 = gather_words(tw2, l_offs2, "v2")
+        vs2 = gather_scales(ts2, l_offs2, "vs2")
+        v3 = gather_words(tw3, l_offs3, "v3")
+        vs3 = gather_scales(ts3, l_offs3, "vs3")
+        w3_d = keep.tile([P, H], I32, name="w3_d", align_bytes=64)
+        deal(w3_d[:], w3_raw[:], 4)
+        ws23_d = keep.tile([P, H], U8, name="ws23_d", align_bytes=64)
+        deal(ws23_d[:], ws23[:], 16)
+        w2_d = keep.tile([P, 2 * H], U8, name="w2_d", align_bytes=64)
+        deal(w2_d[:].bitcast(U16), w2_raw[:].bitcast(U16), 8)
+        gain_turn = keep.tile([P, SLICES], F32, name="gain_turn")
+        nc.vector.tensor_scalar(gain_turn[:], gain_sb[:], TWO_PI, None, ALU.mult)
+
+        work = keep.tile([P, 2 * SLICES + 1, PJ], F32, name="work")
+        GAP = SLICES + 1
+        windows = {}
+        trig = {}
+
+        def bank(name):
+            return psum.tile([P, BANK], F32, name=name, tag="first", bufs=4)
+
+        def first_stage(s):
+            g, t = divmod(s, 4)
+            cols = slice(P * t, P * (t + 1))
+            allc = slice(P * s, P * (s + 1))
+            win_a = ring.tile([P, S], F32, name=f"win_a{s}", tag="win_a")
+            win_d = ring.tile([P, S], F32, name=f"win_d{s}", tag="win_d")
+            win_b = ring.tile([P, S], F32, name=f"win_b{s}", tag="win_b", bufs=3)
+            for h in range(2):
+                m = slice(BANK * h, BANK * (h + 1))
+                acc = bank(f"a{s}{h}")
+                for a, v in enumerate((v10, v11)):
+                    codes, scales = w1_q[a, g]
+                    nc.tensor.matmul_mx(
+                        acc[:], lhsT=codes[:, cols].bitcast(FP8X4), lhsT_scale=scales[:, cols],
+                        rhs=v[:, m].bitcast(FP8X4), rhs_scale=vs1[4 * a : P, m], start=(a == 0), stop=(a == 1),
+                    )
+                nc.scalar.activation(win_a[:, m], acc[:], ACT.Copy, scale=1.0 / TWO_PI)
+            for h in range(2):
+                m = slice(BANK * h, BANK * (h + 1))
+                acc = bank(f"d{s}{h}")
+                nc.tensor.matmul_mx(
+                    acc[:], lhsT=w3_d[:, allc].bitcast(FP8X4), lhsT_scale=ws23_d[4:P, allc],
+                    rhs=v3[:, m].bitcast(FP8X4), rhs_scale=vs3[:, m], start=True, stop=True,
+                )
+                nc.scalar.activation(win_d[:, m], acc[:], ACT.Copy, scale=1.0 / TWO_PI, bias=0.25)
+            for h in range(2):
+                m = slice(BANK * h, BANK * (h + 1))
+                acc = bank(f"b{s}{h}")
+                nc.tensor.matmul_mx(
+                    acc[:], lhsT=w2_d[:, 2 * P * s : 2 * P * (s + 1)].bitcast(FP4X4), lhsT_scale=ws23_d[:, allc],
+                    rhs=v2[:, m].bitcast(FP8X4), rhs_scale=vs2[:, m], start=True, stop=True,
+                )
+                nc.scalar.activation(win_b[:, m], acc[:], ACT.Copy, scale=gain_sb[:, s : s + 1])
+            windows[s] = (win_a, win_b, win_d)
+
+        def angles(s):
+            win_a, win_b, win_d = windows[s]
+            nc.vector.tensor_copy(work[:, s + GAP, :], win_a[:].indirect(l_pos1[:]))
+            nc.vector.tensor_copy(work[:, s, :], win_d[:].indirect(l_pos3[:]))
+            turns = work[:, s : s + GAP + 1 : GAP, :]
+            whole = ring.tile([P, 2, PJ], I32, name=f"whole{s}", tag="whole", bufs=1)
+            nc.vector.tensor_copy(whole[:], turns)
+            frac = ring.tile([P, 2, PJ], F32, name=f"frac{s}", tag="frac")
+            nc.vector.tensor_tensor(frac[:], turns, whole[:], ALU.subtract)
+            nc.scalar.activation(frac[:], frac[:], ACT.Sin, scale=TWO_PI)
+            trig[s] = frac
+
+        def products(s):
+            win_b = windows[s][1]
+            nc.vector.tensor_tensor(work[:, s + 1, :], win_b[:].indirect(l_pos2[:]), trig[s][:, 1, :], ALU.mult)
+            nc.vector.scalar_tensor_tensor(
+                work[:, s + GAP, :], trig[s][:, 0, :], gain_turn[:, s : s + 1], work[:, s + GAP, :], ALU.mult, ALU.mult
+            )
+
+        def join(g, j0, width, zb):
+            js = slice(j0, j0 + width)
+            nc.vector.tensor_tensor(
+                zb[:, 0, :].rearrange("p (c i t) -> p c t i", i=2, t=4),
+                work[:, 4 * g + 1 : 4 * g + 5, js].rearrange("p t (c i) -> p c t i", i=2),
+                work[:, 4 * g + GAP : 4 * g + GAP + 4, js].rearrange("p t (c i) -> p c t i", i=2),
+                ALU.add,
+            )
+            nc.scalar.activation(zb[:, 1, :], zb[:, 0, :], ACT.Abs)
+
+        y_acc = [psum.tile([P, 4, JB], F32, name=f"y_acc{jb}") for jb in range(PJ // JB)]
+
+        def second_stage(g, jb, zq, c0, width):
+            codes, scales = zq
+            for t in range(4):
+                cols = slice(P * t, P * (t + 1))
+                wc = N * g + P * t
+                zc = slice(c0, c0 + JB)
+                ac = slice(width + c0, width + c0 + JB)
+                nc.tensor.matmul_mx(
+                    y_acc[jb][:, t, :], lhsT=w4_d[:, 2 * wc : 2 * wc + 2 * P].bitcast(FP4X4), lhsT_scale=ws4_d[:, wc : wc + P],
+                    rhs=codes[:, zc].bitcast(FP8X4), rhs_scale=scales[:, zc], start=(g == 0 and t == 0), stop=False,
+                )
+                nc.tensor.matmul_mx(
+                    y_acc[jb][:, t, :], lhsT=w5_q[g][0][:, cols].bitcast(FP8X4), lhsT_scale=w5_q[g][1][:, cols],
+                    rhs=codes[:, ac].bitcast(FP8X4), rhs_scale=scales[:, ac], start=False, stop=(g == 1 and t == 3),
+                )
+
+        first_stage(0)
+        angles(0)
+        first_stage(1)
+        w5_q = []
+        for s in range(SLICES):
+            if s + 1 < SLICES:
+                angles(s + 1)
+            if s < 2:
+                w1_q[s, 1] = quantize(round_weight(w1_raw[s, 1], f"w1b{s}1")[:], BANK, f"w1q{s}1")
+            if s in (2, 3):
+                w5_q.append(quantize(round_weight(w5_raw[s - 2], f"w5b{s}")[:], N, f"w5q{s}"))
+            if s == 2:
+                w4_d = keep.tile([P, 4 * N], U8, name="w4_d", align_bytes=64)
+                deal(w4_d[:].bitcast(U16), w4_raw[:].rearrange("p a c -> p (a c)").bitcast(U16), 8)
+                ws4_d = keep.tile([P, 2 * N], U8, name="ws4_d", align_bytes=64)
+                deal(ws4_d[:], ws4[:], 16)
+            if s + 2 < SLICES:
+                first_stage(s + 2)
+            products(s)
+            if s == 3:
+                zb0 = big([P, 2, 4 * PJ], BF16, "zb0")
+                join(0, 0, PJ, zb0)
+            if s == 4:
+                zq0 = quantize(zb0[:].rearrange("p a c -> p (a c)"), 2 * PJ, "zq0")
+                for jb in range(PJ // JB):
+                    second_stage(0, jb, zq0, JB * jb, PJ)
+
+        zb1 = []
+        for jb in range(PJ // JB):
+            zb1.append(ring.tile([P, 2, 4 * JB], BF16, name=f"zb1{jb}", tag="zb1", bufs=4, align_bytes=64))
+            join(1, JB * jb, JB, zb1[jb])
+        for jb in range(PJ // JB):
+            zq1 = quantize(zb1[jb][:].rearrange("p a c -> p (a c)"), 2 * JB, f"zq1{jb}")
+            second_stage(1, jb, zq1, 0, JB)
+
+        y_codes = keep.tile([P, PJ], U32, name="y_codes", align_bytes=64)
+        y_scales = keep.tile([P, PJ], U8, name="y_scales", align_bytes=64)
+        out_rows = out_0.rearrange("(p t) j -> p t j", t=4)
+        out_words = out_1[0].rearrange("p m t -> p (m t)").bitcast(I32)
+        for jb in range(PJ // JB):
+            js = slice(JB * jb, JB * (jb + 1))
+            y_sb = ring.tile([P, 4, JB], F32, name=f"y_sb{jb}", tag="y_sb", bufs=4)
+            nc.scalar.copy(y_sb[:], y_acc[jb][:])
+            nc.sync.dma_start(out_rows[:, :, js], y_sb[:])
+            yb = ring.tile([P, 4 * JB], BF16, name=f"yb{jb}", tag="yb", align_bytes=64)
+            nc.vector.tensor_copy(
+                yb[:].rearrange("p (c i t) -> p c t i", i=2, t=4),
+                y_sb[:].rearrange("p t (c i) -> p c t i", i=2),
+            )
+            nc.vector.quantize_mx(out=y_codes[:, js].bitcast(FP8X4), scales=y_scales[:, js], in_=yb[:])
+            nc.sync.dma_start(out_words[:, js], y_codes[:, js].bitcast(I32))
+        for q in range(4):
+            queue = nc.sync if q % 2 == 0 else nc.scalar
+            queue.dma_start(out_2[0, 4 * q : 4 * q + 4, :].bitcast(I32), y_scales[32 * q : 32 * q + 4, :].bitcast(I32))

@@ -59,9 +59,9 @@ def tile_list_holding_stack_features_kernel(
             nc.vector.memset(t[:].bitcast(I32), 0)
             return t
 
-        def load_scale_rows(queue, plane, scales, first_row):
+        def load_scale_rows(queue, plane, scales, first_row, quadrants=(0, 1, 2, 3)):
             rows = 4 * scales.shape[0]
-            for q in range(4):
+            for q in quadrants:
                 p0 = 32 * q + first_row
                 queue.dma_start(plane[p0 : p0 + rows, :].bitcast(I32), scales[:, 4 * q : 4 * q + 4, :].bitcast(I32))
 
@@ -70,9 +70,6 @@ def tile_list_holding_stack_features_kernel(
         ts3 = zeroed_plane(T, "ts3")
         ws23 = zeroed_plane(H, "ws23")
         ws4 = zeroed_plane(2 * N, "ws4")
-        load_scale_rows(nc.scalar, ts1, tab_scales, 0)
-        load_scale_rows(nc.scalar, ts2, tab2_scales, 0)
-        load_scale_rows(nc.scalar, ts3, tab3_scales, 0)
         load_scale_rows(nc.gpsimd, ws23, w2_scales, 0)
         load_scale_rows(nc.gpsimd, ws23, w3_scales, 4)
         for q in range(4):
@@ -83,23 +80,31 @@ def tile_list_holding_stack_features_kernel(
 
         l_offs = load_list(offs, "l_offs")
         tw10 = load_table_words(tab_words, 0, "tw10")
-        tw11 = load_table_words(tab_words, 1, "tw11")
-        w1_raw = {}
-        for a in range(2):
-            w1_raw[a, 0] = load_weight_rows(w1, a, 0, f"w1r{a}0")
-        l_offs2 = load_list(offs2, "l_offs2")
-        tw2 = load_table_words(tab2_words, 0, "tw2")
-        w2_raw = keep.tile([P, 2 * H], U8, name="w2_raw")
-        nc.sync.dma_start(w2_raw[:].bitcast(I32), w2_words[0].bitcast(I32))
         l_offs3 = load_list(offs3, "l_offs3")
+        tw11 = load_table_words(tab_words, 1, "tw11")
+        l_offs2 = load_list(offs2, "l_offs2")
         tw3 = load_table_words(tab3_words, 0, "tw3")
-        w3_raw = keep.tile([P, H], I32, name="w3_raw")
-        nc.sync.dma_start(w3_raw[:], w3_words[0].rearrange("p c i -> p (c i)").bitcast(I32))
         l_pos1 = load_list(pos1, "l_pos1")
         l_pos3 = load_list(pos3, "l_pos3")
-        l_pos2 = load_list(pos2, "l_pos2")
+        w1_raw = {}
+        load_scale_rows(nc.sync, ts1, tab_scales, 0, (0,))
+        w1_raw[0, 0] = load_weight_rows(w1, 0, 0, "w1r00")
+        load_scale_rows(nc.sync, ts1, tab_scales, 0, (1,))
+        w1_raw[1, 0] = load_weight_rows(w1, 1, 0, "w1r10")
+        load_scale_rows(nc.sync, ts1, tab_scales, 0, (2,))
+        w3_raw = keep.tile([P, H], I32, name="w3_raw")
+        nc.sync.dma_start(w3_raw[:], w3_words[0].rearrange("p c i -> p (c i)").bitcast(I32))
+        load_scale_rows(nc.sync, ts1, tab_scales, 0, (3,))
+        load_scale_rows(nc.sync, ts3, tab3_scales, 0, (0, 1))
+        tw2 = load_table_words(tab2_words, 0, "tw2")
+        load_scale_rows(nc.sync, ts3, tab3_scales, 0, (2,))
+        w2_raw = keep.tile([P, 2 * H], U8, name="w2_raw")
+        nc.sync.dma_start(w2_raw[:].bitcast(I32), w2_words[0].bitcast(I32))
+        load_scale_rows(nc.sync, ts3, tab3_scales, 0, (3,))
+        load_scale_rows(nc.sync, ts2, tab2_scales, 0)
         gain_sb = keep.tile([P, SLICES], F32, name="gain_sb")
         nc.sync.dma_start(gain_sb[:].rearrange("p (g t) -> p g t", t=4), gain.rearrange("(g p t) -> p g t", p=P, t=4))
+        l_pos2 = load_list(pos2, "l_pos2")
         for a in range(2):
             w1_raw[a, 1] = load_weight_rows(w1, a, BANK, f"w1r{a}1")
         w4_raw = keep.tile([P, 2, 2 * N], U8, name="w4_raw")
@@ -143,14 +148,14 @@ def tile_list_holding_stack_features_kernel(
         w1_q = {}
         for a in range(2):
             w1_q[a, 0] = quantize(round_weight(w1_raw[a, 0], f"w1b{a}0")[:], BANK, f"w1q{a}0")
-        v2 = gather_words(tw2, l_offs2, "v2")
-        vs2 = gather_scales(ts2, l_offs2, "vs2")
         v3 = gather_words(tw3, l_offs3, "v3")
         vs3 = gather_scales(ts3, l_offs3, "vs3")
         w3_d = keep.tile([P, H], I32, name="w3_d", align_bytes=64)
         deal(w3_d[:], w3_raw[:], 4)
         ws23_d = keep.tile([P, H], U8, name="ws23_d", align_bytes=64)
         deal(ws23_d[:], ws23[:], 16)
+        v2 = gather_words(tw2, l_offs2, "v2")
+        vs2 = gather_scales(ts2, l_offs2, "vs2")
         w2_d = keep.tile([P, 2 * H], U8, name="w2_d", align_bytes=64)
         deal(w2_d[:].bitcast(U16), w2_raw[:].bitcast(U16), 8)
         gain_turn = keep.tile([P, SLICES], F32, name="gain_turn")
@@ -160,17 +165,21 @@ def tile_list_holding_stack_features_kernel(
         GAP = SLICES + 1
         windows = {}
         trig = {}
+        whole = {}
 
         def bank(name):
             return psum.tile([P, BANK], F32, name=name, tag="first", bufs=4)
+
+        def slot_tile(shape, dtype, name, slot):
+            return ring.tile(shape, dtype, name=name, tag=f"slot{slot % 4}", bufs=1)
 
         def first_stage(s):
             g, t = divmod(s, 4)
             cols = slice(P * t, P * (t + 1))
             allc = slice(P * s, P * (s + 1))
             win_a = ring.tile([P, S], F32, name=f"win_a{s}", tag="win_a")
-            win_d = ring.tile([P, S], F32, name=f"win_d{s}", tag="win_d")
-            win_b = ring.tile([P, S], F32, name=f"win_b{s}", tag="win_b", bufs=3)
+            win_d = slot_tile([P, S], F32, f"win_d{s}", s)
+            win_b = ring.tile([P, S], F32, name=f"win_b{s}", tag="win_b", bufs=4)
             for h in range(2):
                 m = slice(BANK * h, BANK * (h + 1))
                 acc = bank(f"a{s}{h}")
@@ -199,15 +208,18 @@ def tile_list_holding_stack_features_kernel(
                 nc.scalar.activation(win_b[:, m], acc[:], ACT.Copy, scale=gain_sb[:, s : s + 1])
             windows[s] = (win_a, win_b, win_d)
 
-        def angles(s):
+        def pick(s):
             win_a, win_b, win_d = windows[s]
             nc.vector.tensor_copy(work[:, s + GAP, :], win_a[:].indirect(l_pos1[:]))
             nc.vector.tensor_copy(work[:, s, :], win_d[:].indirect(l_pos3[:]))
-            turns = work[:, s : s + GAP + 1 : GAP, :]
-            whole = ring.tile([P, 2, PJ], I32, name=f"whole{s}", tag="whole", bufs=1)
-            nc.vector.tensor_copy(whole[:], turns)
-            frac = ring.tile([P, 2, PJ], F32, name=f"frac{s}", tag="frac")
-            nc.vector.tensor_tensor(frac[:], turns, whole[:], ALU.subtract)
+
+        def whole_turns(s):
+            whole[s] = slot_tile([P, 2, PJ], I32, f"whole{s}", s - 1)
+            nc.gpsimd.tensor_scalar(whole[s][:], work[:, s : s + GAP + 1 : GAP, :], 1.0, 0.0, ALU.mult, ALU.add)
+
+        def angles(s):
+            frac = slot_tile([P, 2, PJ], F32, f"frac{s}", s + 1)
+            nc.vector.tensor_tensor(frac[:], work[:, s : s + GAP + 1 : GAP, :], whole[s][:], ALU.subtract)
             nc.scalar.activation(frac[:], frac[:], ACT.Sin, scale=TWO_PI)
             trig[s] = frac
 
@@ -247,28 +259,32 @@ def tile_list_holding_stack_features_kernel(
                 )
 
         first_stage(0)
-        angles(0)
         first_stage(1)
         w5_q = []
-        for s in range(SLICES):
-            if s + 1 < SLICES:
-                angles(s + 1)
-            if s < 2:
-                w1_q[s, 1] = quantize(round_weight(w1_raw[s, 1], f"w1b{s}1")[:], BANK, f"w1q{s}1")
-            if s in (2, 3):
-                w5_q.append(quantize(round_weight(w5_raw[s - 2], f"w5b{s}")[:], N, f"w5q{s}"))
-            if s == 2:
+        for i in range(SLICES + 2):
+            if i < SLICES:
+                pick(i)
+            if 1 <= i <= SLICES:
+                angles(i - 1)
+            if i < 2:
+                w1_q[i, 1] = quantize(round_weight(w1_raw[i, 1], f"w1b{i}1")[:], BANK, f"w1q{i}1")
+            if i in (3, 4):
+                w5_q.append(quantize(round_weight(w5_raw[i - 3], f"w5b{i}")[:], N, f"w5q{i}"))
+            if i == 4:
                 w4_d = keep.tile([P, 4 * N], U8, name="w4_d", align_bytes=64)
                 deal(w4_d[:].bitcast(U16), w4_raw[:].rearrange("p a c -> p (a c)").bitcast(U16), 8)
                 ws4_d = keep.tile([P, 2 * N], U8, name="ws4_d", align_bytes=64)
                 deal(ws4_d[:], ws4[:], 16)
-            if s + 2 < SLICES:
-                first_stage(s + 2)
-            products(s)
-            if s == 3:
+            if i + 2 < SLICES:
+                first_stage(i + 2)
+            if i >= 2:
+                products(i - 2)
+            if i < SLICES:
+                whole_turns(i)
+            if i == 5:
                 zb0 = big([P, 2, 4 * PJ], BF16, "zb0")
                 join(0, 0, PJ, zb0)
-            if s == 4:
+            if i == 6:
                 zq0 = quantize(zb0[:].rearrange("p a c -> p (a c)"), 2 * PJ, "zq0")
                 for jb in range(PJ // JB):
                     second_stage(0, jb, zq0, JB * jb, PJ)

@@ -80,33 +80,28 @@ def tile_list_holding_stack_features_kernel(
 
         l_offs = load_list(offs, "l_offs")
         tw10 = load_table_words(tab_words, 0, "tw10")
-        l_offs3 = load_list(offs3, "l_offs3")
+        load_scale_rows(nc.sync, ts1, tab_scales, 0)
         tw11 = load_table_words(tab_words, 1, "tw11")
-        l_offs2 = load_list(offs2, "l_offs2")
-        tw3 = load_table_words(tab3_words, 0, "tw3")
-        l_pos1 = load_list(pos1, "l_pos1")
-        l_pos3 = load_list(pos3, "l_pos3")
         w1_raw = {}
-        load_scale_rows(nc.sync, ts1, tab_scales, 0, (0,))
         w1_raw[0, 0] = load_weight_rows(w1, 0, 0, "w1r00")
-        load_scale_rows(nc.sync, ts1, tab_scales, 0, (1,))
+        l_offs3 = load_list(offs3, "l_offs3")
         w1_raw[1, 0] = load_weight_rows(w1, 1, 0, "w1r10")
-        load_scale_rows(nc.sync, ts1, tab_scales, 0, (2,))
-        w3_raw = keep.tile([P, H], I32, name="w3_raw")
+        load_scale_rows(nc.sync, ts3, tab3_scales, 0)
+        tw3 = load_table_words(tab3_words, 0, "tw3")
+        w1_raw[0, 1] = load_weight_rows(w1, 0, BANK, "w1r01")
+        l_offs2 = load_list(offs2, "l_offs2")
+        w3_raw = keep.tile([P, H], I32, name="w3_raw", tag="w3_then_w4", align_bytes=64)
         nc.sync.dma_start(w3_raw[:], w3_words[0].rearrange("p c i -> p (c i)").bitcast(I32))
-        load_scale_rows(nc.sync, ts1, tab_scales, 0, (3,))
-        load_scale_rows(nc.sync, ts3, tab3_scales, 0, (0, 1))
-        tw2 = load_table_words(tab2_words, 0, "tw2")
-        load_scale_rows(nc.sync, ts3, tab3_scales, 0, (2,))
-        w2_raw = keep.tile([P, 2 * H], U8, name="w2_raw")
-        nc.sync.dma_start(w2_raw[:].bitcast(I32), w2_words[0].bitcast(I32))
-        load_scale_rows(nc.sync, ts3, tab3_scales, 0, (3,))
         load_scale_rows(nc.sync, ts2, tab2_scales, 0)
+        tw2 = load_table_words(tab2_words, 0, "tw2")
+        w1_raw[1, 1] = load_weight_rows(w1, 1, BANK, "w1r11")
+        l_pos1 = load_list(pos1, "l_pos1")
+        w2_raw = keep.tile([P, 2 * H], U8, name="w2_raw", tag="w2_then_ws4", align_bytes=64)
+        nc.sync.dma_start(w2_raw[:].bitcast(I32), w2_words[0].bitcast(I32))
+        l_pos3 = load_list(pos3, "l_pos3")
         gain_sb = keep.tile([P, SLICES], F32, name="gain_sb")
         nc.sync.dma_start(gain_sb[:].rearrange("p (g t) -> p g t", t=4), gain.rearrange("(g p t) -> p g t", p=P, t=4))
         l_pos2 = load_list(pos2, "l_pos2")
-        for a in range(2):
-            w1_raw[a, 1] = load_weight_rows(w1, a, BANK, f"w1r{a}1")
         w4_raw = keep.tile([P, 2, 2 * N], U8, name="w4_raw")
         nc.sync.dma_start(w4_raw[:].bitcast(I32), w4_words.bitcast(I32).rearrange("a p c -> p a c"))
         w5_raw = [load_weight_rows(w5, g, 0, f"w5r{g}") for g in range(2)]
@@ -148,14 +143,14 @@ def tile_list_holding_stack_features_kernel(
         w1_q = {}
         for a in range(2):
             w1_q[a, 0] = quantize(round_weight(w1_raw[a, 0], f"w1b{a}0")[:], BANK, f"w1q{a}0")
-        v3 = gather_words(tw3, l_offs3, "v3")
         vs3 = gather_scales(ts3, l_offs3, "vs3")
+        v3 = gather_words(tw3, l_offs3, "v3")
+        vs2 = gather_scales(ts2, l_offs2, "vs2")
         w3_d = keep.tile([P, H], I32, name="w3_d", align_bytes=64)
         deal(w3_d[:], w3_raw[:], 4)
-        ws23_d = keep.tile([P, H], U8, name="ws23_d", align_bytes=64)
+        ws23_d = keep.tile([P, H], U8, name="ws23_d", tag="ts2", align_bytes=64)
         deal(ws23_d[:], ws23[:], 16)
         v2 = gather_words(tw2, l_offs2, "v2")
-        vs2 = gather_scales(ts2, l_offs2, "vs2")
         w2_d = keep.tile([P, 2 * H], U8, name="w2_d", align_bytes=64)
         deal(w2_d[:].bitcast(U16), w2_raw[:].bitcast(U16), 8)
         gain_turn = keep.tile([P, SLICES], F32, name="gain_turn")
@@ -168,7 +163,7 @@ def tile_list_holding_stack_features_kernel(
         whole = {}
 
         def bank(name):
-            return psum.tile([P, BANK], F32, name=name, tag="first", bufs=4)
+            return psum.tile([P, BANK], F32, name=name, tag="bank", bufs=8)
 
         def slot_tile(shape, dtype, name, slot):
             return ring.tile(shape, dtype, name=name, tag=f"slot{slot % 4}", bufs=1)
@@ -177,7 +172,7 @@ def tile_list_holding_stack_features_kernel(
             g, t = divmod(s, 4)
             cols = slice(P * t, P * (t + 1))
             allc = slice(P * s, P * (s + 1))
-            win_a = ring.tile([P, S], F32, name=f"win_a{s}", tag="win_a")
+            win_a = ring.tile([P, S], F32, name=f"win_a{s}", tag="win_a", bufs=3)
             win_d = slot_tile([P, S], F32, f"win_d{s}", s)
             win_b = ring.tile([P, S], F32, name=f"win_b{s}", tag="win_b", bufs=4)
             for h in range(2):
@@ -215,7 +210,10 @@ def tile_list_holding_stack_features_kernel(
 
         def whole_turns(s):
             whole[s] = slot_tile([P, 2, PJ], I32, f"whole{s}", s - 1)
-            nc.gpsimd.tensor_scalar(whole[s][:], work[:, s : s + GAP + 1 : GAP, :], 1.0, 0.0, ALU.mult, ALU.add)
+            if s + 1 < SLICES:
+                nc.gpsimd.tensor_scalar(whole[s][:], work[:, s : s + GAP + 1 : GAP, :], 1.0, 0.0, ALU.mult, ALU.add)
+            else:
+                nc.vector.tensor_copy(whole[s][:], work[:, s : s + GAP + 1 : GAP, :])
 
         def angles(s):
             frac = slot_tile([P, 2, PJ], F32, f"frac{s}", s + 1)
@@ -240,7 +238,7 @@ def tile_list_holding_stack_features_kernel(
             )
             nc.scalar.activation(zb[:, 1, :], zb[:, 0, :], ACT.Abs)
 
-        y_acc = [psum.tile([P, 4, JB], F32, name=f"y_acc{jb}") for jb in range(PJ // JB)]
+        y_acc = []
 
         def second_stage(g, jb, zq, c0, width):
             codes, scales = zq
@@ -259,6 +257,8 @@ def tile_list_holding_stack_features_kernel(
                 )
 
         first_stage(0)
+        for a in range(2):
+            w1_q[a, 1] = quantize(round_weight(w1_raw[a, 1], f"w1b{a}1")[:], BANK, f"w1q{a}1")
         first_stage(1)
         w5_q = []
         for i in range(SLICES + 2):
@@ -266,14 +266,10 @@ def tile_list_holding_stack_features_kernel(
                 pick(i)
             if 1 <= i <= SLICES:
                 angles(i - 1)
-            if i < 2:
-                w1_q[i, 1] = quantize(round_weight(w1_raw[i, 1], f"w1b{i}1")[:], BANK, f"w1q{i}1")
-            if i in (3, 4):
-                w5_q.append(quantize(round_weight(w5_raw[i - 3], f"w5b{i}")[:], N, f"w5q{i}"))
             if i == 4:
-                w4_d = keep.tile([P, 4 * N], U8, name="w4_d", align_bytes=64)
+                w4_d = keep.tile([P, 4 * N], U8, name="w4_d", tag="w3_then_w4", align_bytes=64)
                 deal(w4_d[:].bitcast(U16), w4_raw[:].rearrange("p a c -> p (a c)").bitcast(U16), 8)
-                ws4_d = keep.tile([P, 2 * N], U8, name="ws4_d", align_bytes=64)
+                ws4_d = keep.tile([P, 2 * N], U8, name="ws4_d", tag="w2_then_ws4", align_bytes=64)
                 deal(ws4_d[:], ws4[:], 16)
             if i + 2 < SLICES:
                 first_stage(i + 2)
@@ -284,18 +280,23 @@ def tile_list_holding_stack_features_kernel(
             if i == 5:
                 zb0 = big([P, 2, 4 * PJ], BF16, "zb0")
                 join(0, 0, PJ, zb0)
+            if i in (6, 7):
+                w5_q.append(quantize(round_weight(w5_raw[i - 6], f"w5b{i}")[:], N, f"w5q{i}"))
             if i == 6:
                 zq0 = quantize(zb0[:].rearrange("p a c -> p (a c)"), 2 * PJ, "zq0")
+            if i == 7:
                 for jb in range(PJ // JB):
+                    y_acc.append(psum.tile([P, 4, JB], F32, name=f"y_acc{jb}", tag="bank", bufs=8))
                     second_stage(0, jb, zq0, JB * jb, PJ)
 
         zb1 = []
-        for jb in range(PJ // JB):
-            zb1.append(ring.tile([P, 2, 4 * JB], BF16, name=f"zb1{jb}", tag="zb1", bufs=4, align_bytes=64))
-            join(1, JB * jb, JB, zb1[jb])
-        for jb in range(PJ // JB):
-            zq1 = quantize(zb1[jb][:].rearrange("p a c -> p (a c)"), 2 * JB, f"zq1{jb}")
-            second_stage(1, jb, zq1, 0, JB)
+        for jb in range(PJ // JB + 1):
+            if jb < PJ // JB:
+                zb1.append(ring.tile([P, 2, 4 * JB], BF16, name=f"zb1{jb}", tag="zb1", bufs=4, align_bytes=64))
+                join(1, JB * jb, JB, zb1[jb])
+            if jb >= 1:
+                zq1 = quantize(zb1[jb - 1][:].rearrange("p a c -> p (a c)"), 2 * JB, f"zq1{jb - 1}")
+                second_stage(1, jb - 1, zq1, 0, JB)
 
         y_codes = keep.tile([P, PJ], U32, name="y_codes", align_bytes=64)
         y_scales = keep.tile([P, PJ], U8, name="y_scales", align_bytes=64)
@@ -312,7 +313,9 @@ def tile_list_holding_stack_features_kernel(
                 y_sb[:].rearrange("p t (c i) -> p c t i", i=2),
             )
             nc.vector.quantize_mx(out=y_codes[:, js].bitcast(FP8X4), scales=y_scales[:, js], in_=yb[:])
-            nc.sync.dma_start(out_words[:, js], y_codes[:, js].bitcast(I32))
+            if jb >= 2:
+                done = slice(0, 3 * JB) if jb == 2 else js
+                nc.scalar.dma_start(out_words[:, done], y_codes[:, done].bitcast(I32))
         for q in range(4):
             queue = nc.sync if q % 2 == 0 else nc.scalar
             queue.dma_start(out_2[0, 4 * q : 4 * q + 4, :].bitcast(I32), y_scales[32 * q : 32 * q + 4, :].bitcast(I32))

@@ -2,6 +2,7 @@ import math
 from contextlib import ExitStack
 
 import concourse.mybir as mybir
+from concourse.masks import make_identity
 
 K, K2, K3, H, N, T, S, PJ = 1024, 512, 512, 1024, 512, 2048, 1024, 512
 FLOPS = 2 * H * S * (K + K2 + K3) + 2 * 2 * H * N * PJ
@@ -22,6 +23,7 @@ BANK = 512
 SLICES = H // P
 TWO_PI = 2.0 * math.pi
 JB = 128
+ROUNDER = 1.5 * 2.0**23
 
 
 def tile_list_holding_stack_features_kernel(
@@ -72,11 +74,6 @@ def tile_list_holding_stack_features_kernel(
         ws4 = zeroed_plane(2 * N, "ws4")
         load_scale_rows(nc.gpsimd, ws23, w2_scales, 0)
         load_scale_rows(nc.gpsimd, ws23, w3_scales, 4)
-        for q in range(4):
-            nc.gpsimd.dma_start(
-                ws4[32 * q : 32 * q + 4, :].bitcast(I32).rearrange("p (a c) -> p a c", a=2),
-                w4_scales[:, 4 * q : 4 * q + 4, :].bitcast(I32).rearrange("a r c -> r a c"),
-            )
 
         l_offs = load_list(offs, "l_offs")
         tw10 = load_table_words(tab_words, 0, "tw10")
@@ -87,24 +84,33 @@ def tile_list_holding_stack_features_kernel(
         l_offs3 = load_list(offs3, "l_offs3")
         w1_raw[1, 0] = load_weight_rows(w1, 1, 0, "w1r10")
         load_scale_rows(nc.sync, ts3, tab3_scales, 0)
-        tw3 = load_table_words(tab3_words, 0, "tw3")
         w1_raw[0, 1] = load_weight_rows(w1, 0, BANK, "w1r01")
+        tw3 = load_table_words(tab3_words, 0, "tw3")
         l_offs2 = load_list(offs2, "l_offs2")
-        w3_raw = keep.tile([P, H], I32, name="w3_raw", tag="w3_then_w4", align_bytes=64)
-        nc.sync.dma_start(w3_raw[:], w3_words[0].rearrange("p c i -> p (c i)").bitcast(I32))
-        load_scale_rows(nc.sync, ts2, tab2_scales, 0)
-        tw2 = load_table_words(tab2_words, 0, "tw2")
         w1_raw[1, 1] = load_weight_rows(w1, 1, BANK, "w1r11")
+        load_scale_rows(nc.sync, ts2, tab2_scales, 0)
+        w3_raw = keep.tile([P, H], I32, name="w3_raw", align_bytes=64)
+        nc.sync.dma_start(w3_raw[:], w3_words[0].rearrange("p c i -> p (c i)").bitcast(I32))
+        w5_raw = [load_weight_rows(w5, 0, 0, "w5r0")]
         l_pos1 = load_list(pos1, "l_pos1")
-        w2_raw = keep.tile([P, 2 * H], U8, name="w2_raw", tag="w2_then_ws4", align_bytes=64)
-        nc.sync.dma_start(w2_raw[:].bitcast(I32), w2_words[0].bitcast(I32))
+        w5_raw.append(load_weight_rows(w5, 1, 0, "w5r1"))
         l_pos3 = load_list(pos3, "l_pos3")
-        gain_sb = keep.tile([P, SLICES], F32, name="gain_sb")
-        nc.sync.dma_start(gain_sb[:].rearrange("p (g t) -> p g t", t=4), gain.rearrange("(g p t) -> p g t", p=P, t=4))
+        tw2 = load_table_words(tab2_words, 0, "tw2")
+        w2_raw = keep.tile([P, 2 * H], U8, name="w2_raw", align_bytes=64)
+        nc.sync.dma_start(w2_raw[:].bitcast(I32), w2_words[0].bitcast(I32))
+        gain_sb = [keep.tile([P, 4], F32, name=f"gain_sb{g}") for g in range(2)]
+        with nc.allow_non_contiguous_dma(reason="one gain value a partition and slice"):
+            nc.sync.dma_start(gain_sb[0][:], gain[0:BANK].rearrange("(t p) -> p t", p=P))
+        nc.sync.dma_start(gain_sb[1][:], gain[BANK:H].rearrange("(p t) -> p t", t=4))
         l_pos2 = load_list(pos2, "l_pos2")
         w4_raw = keep.tile([P, 2, 2 * N], U8, name="w4_raw")
         nc.sync.dma_start(w4_raw[:].bitcast(I32), w4_words.bitcast(I32).rearrange("a p c -> p a c"))
-        w5_raw = [load_weight_rows(w5, g, 0, f"w5r{g}") for g in range(2)]
+
+        for q in range(4):
+            nc.sync.dma_start(
+                ws4[32 * q : 32 * q + 4, :].bitcast(I32).rearrange("p (a c) -> p a c", a=2),
+                w4_scales[:, 4 * q : 4 * q + 4, :].bitcast(I32).rearrange("a r c -> r a c"),
+            )
 
         def gather_words(table, offsets, name):
             t = keep.tile([P, S], U32, name=name, align_bytes=64)
@@ -116,18 +122,24 @@ def tile_list_holding_stack_features_kernel(
             nc.vector.tensor_copy(t[:], plane[:].indirect(offsets[:]))
             return t
 
-        def deal(dst, src, run):
+        def deal(dst, src, run, groups=2):
             nc.vector.tensor_copy(
-                dst.rearrange("p (g t c i) -> p g c t i", g=2, t=4, i=run),
-                src.rearrange("p (g c i t) -> p g c t i", g=2, t=4, i=run),
+                dst.rearrange("p (g t c i) -> p g c t i", g=groups, t=4, i=run),
+                src.rearrange("p (g c i t) -> p g c t i", g=groups, t=4, i=run),
             )
 
-        def round_weight(raw, name):
+        def round_weight(raw, name, dealt=False):
             wb = ring.tile([P, 4 * BANK], BF16, name=name, tag="wb", align_bytes=64)
-            nc.scalar.copy(
-                wb[:].rearrange("p (t q j) -> p q j t", t=4, j=4),
-                raw[:].rearrange("p j (q t) -> p q j t", t=4),
-            )
+            if dealt:
+                nc.scalar.copy(
+                    wb[:].rearrange("p (t q j) -> p q j t", t=4, j=4),
+                    raw[:].rearrange("p j (q t) -> p q j t", t=4),
+                )
+            else:
+                nc.scalar.copy(
+                    wb[:].rearrange("p (c i j) -> p c j i", i=4, j=4),
+                    raw[:].rearrange("p j (c i) -> p c j i", i=4),
+                )
             return wb
 
         def quantize(src, width, name, pool=keep, tag=None, bufs=None):
@@ -144,37 +156,34 @@ def tile_list_holding_stack_features_kernel(
         for a in range(2):
             w1_q[a, 0] = quantize(round_weight(w1_raw[a, 0], f"w1b{a}0")[:], BANK, f"w1q{a}0")
         vs3 = gather_scales(ts3, l_offs3, "vs3")
-        v3 = gather_words(tw3, l_offs3, "v3")
         vs2 = gather_scales(ts2, l_offs2, "vs2")
-        w3_d = keep.tile([P, H], I32, name="w3_d", align_bytes=64)
-        deal(w3_d[:], w3_raw[:], 4)
-        ws23_d = keep.tile([P, H], U8, name="ws23_d", tag="ts2", align_bytes=64)
-        deal(ws23_d[:], ws23[:], 16)
+        for a in range(2):
+            w1_q[a, 1] = quantize(round_weight(w1_raw[a, 1], f"w1b{a}1", dealt=True)[:], BANK, f"w1q{a}1")
+        v3 = gather_words(tw3, l_offs3, "v3")
         v2 = gather_words(tw2, l_offs2, "v2")
-        w2_d = keep.tile([P, 2 * H], U8, name="w2_d", align_bytes=64)
-        deal(w2_d[:].bitcast(U16), w2_raw[:].bitcast(U16), 8)
         gain_turn = keep.tile([P, SLICES], F32, name="gain_turn")
-        nc.vector.tensor_scalar(gain_turn[:], gain_sb[:], TWO_PI, None, ALU.mult)
+        for g in range(2):
+            nc.scalar.activation(gain_turn[:, 4 * g : 4 * g + 4], gain_sb[g][:], ACT.Copy, scale=TWO_PI)
 
         work = keep.tile([P, 2 * SLICES + 1, PJ], F32, name="work")
         GAP = SLICES + 1
         windows = {}
+        windows_b = {}
         trig = {}
         whole = {}
 
         def bank(name):
-            return psum.tile([P, BANK], F32, name=name, tag="bank", bufs=8)
+            return psum.tile([P, BANK], F32, name=name, tag="bank", bufs=6)
 
         def slot_tile(shape, dtype, name, slot):
-            return ring.tile(shape, dtype, name=name, tag=f"slot{slot % 4}", bufs=1)
+            return ring.tile(shape, dtype, name=name, tag=f"slot{slot % 3}", bufs=1)
 
         def first_stage(s):
             g, t = divmod(s, 4)
             cols = slice(P * t, P * (t + 1))
-            allc = slice(P * s, P * (s + 1))
+            w2_g, w3_g, ws23_g = packed[g]
             win_a = ring.tile([P, S], F32, name=f"win_a{s}", tag="win_a", bufs=3)
             win_d = slot_tile([P, S], F32, f"win_d{s}", s)
-            win_b = ring.tile([P, S], F32, name=f"win_b{s}", tag="win_b", bufs=4)
             for h in range(2):
                 m = slice(BANK * h, BANK * (h + 1))
                 acc = bank(f"a{s}{h}")
@@ -189,54 +198,77 @@ def tile_list_holding_stack_features_kernel(
                 m = slice(BANK * h, BANK * (h + 1))
                 acc = bank(f"d{s}{h}")
                 nc.tensor.matmul_mx(
-                    acc[:], lhsT=w3_d[:, allc].bitcast(FP8X4), lhsT_scale=ws23_d[4:P, allc],
+                    acc[:], lhsT=w3_g[:, cols].bitcast(FP8X4), lhsT_scale=ws23_g[4:P, cols],
                     rhs=v3[:, m].bitcast(FP8X4), rhs_scale=vs3[:, m], start=True, stop=True,
                 )
                 nc.scalar.activation(win_d[:, m], acc[:], ACT.Copy, scale=1.0 / TWO_PI, bias=0.25)
+            windows[s] = (win_a, win_d)
+
+        def first_stage_b(s):
+            g, t = divmod(s, 4)
+            cols = slice(P * t, P * (t + 1))
+            w2_g, w3_g, ws23_g = packed[g]
+            win_b = ring.tile([P, S], F32, name=f"win_b{s}", tag="win_b", bufs=3)
             for h in range(2):
                 m = slice(BANK * h, BANK * (h + 1))
                 acc = bank(f"b{s}{h}")
                 nc.tensor.matmul_mx(
-                    acc[:], lhsT=w2_d[:, 2 * P * s : 2 * P * (s + 1)].bitcast(FP4X4), lhsT_scale=ws23_d[:, allc],
+                    acc[:], lhsT=w2_g[:, 2 * P * t : 2 * P * (t + 1)].bitcast(FP4X4), lhsT_scale=ws23_g[:, cols],
                     rhs=v2[:, m].bitcast(FP8X4), rhs_scale=vs2[:, m], start=True, stop=True,
                 )
-                nc.scalar.activation(win_b[:, m], acc[:], ACT.Copy, scale=gain_sb[:, s : s + 1])
-            windows[s] = (win_a, win_b, win_d)
+                nc.scalar.activation(win_b[:, m], acc[:], ACT.Copy, scale=gain_sb[g][:, t : t + 1])
+            windows_b[s] = win_b
 
         def pick(s):
-            win_a, win_b, win_d = windows[s]
+            win_a, win_d = windows[s]
             nc.vector.tensor_copy(work[:, s + GAP, :], win_a[:].indirect(l_pos1[:]))
             nc.vector.tensor_copy(work[:, s, :], win_d[:].indirect(l_pos3[:]))
 
         def whole_turns(s):
-            whole[s] = slot_tile([P, 2, PJ], I32, f"whole{s}", s - 1)
-            if s + 1 < SLICES:
-                nc.gpsimd.tensor_scalar(whole[s][:], work[:, s : s + GAP + 1 : GAP, :], 1.0, 0.0, ALU.mult, ALU.add)
+            whole[s] = ring.tile([P, 2, PJ], I32, name=f"whole{s}", tag="whole")
+            turns = work[:, s : s + GAP + 1 : GAP, :]
+            if s < 6:
+                nc.scalar.activation(whole[s][:].bitcast(U32), turns, ACT.Copy, bias=ROUNDER)
             else:
-                nc.vector.tensor_copy(whole[s][:], work[:, s : s + GAP + 1 : GAP, :])
+                nc.vector.tensor_scalar(whole[s][:], turns, ROUNDER, None, ALU.add)
 
         def angles(s):
             frac = slot_tile([P, 2, PJ], F32, f"frac{s}", s + 1)
-            nc.vector.tensor_tensor(frac[:], work[:, s : s + GAP + 1 : GAP, :], whole[s][:], ALU.subtract)
-            nc.scalar.activation(frac[:], frac[:], ACT.Sin, scale=TWO_PI)
+            nc.vector.scalar_tensor_tensor(
+                frac[:], whole[s][:], ROUNDER, work[:, s : s + GAP + 1 : GAP, :], ALU.subtract, ALU.subtract
+            )
+            nc.scalar.activation(frac[:], frac[:], ACT.Sin, scale=-TWO_PI)
             trig[s] = frac
 
         def products(s):
-            win_b = windows[s][1]
+            win_b = windows_b[s]
             nc.vector.tensor_tensor(work[:, s + 1, :], win_b[:].indirect(l_pos2[:]), trig[s][:, 1, :], ALU.mult)
             nc.vector.scalar_tensor_tensor(
                 work[:, s + GAP, :], trig[s][:, 0, :], gain_turn[:, s : s + 1], work[:, s + GAP, :], ALU.mult, ALU.mult
             )
 
-        def join(g, j0, width, zb):
-            js = slice(j0, j0 + width)
-            nc.vector.tensor_tensor(
-                zb[:, 0, :].rearrange("p (c i t) -> p c t i", i=2, t=4),
-                work[:, 4 * g + 1 : 4 * g + 5, js].rearrange("p t (c i) -> p c t i", i=2),
-                work[:, 4 * g + GAP : 4 * g + GAP + 4, js].rearrange("p t (c i) -> p c t i", i=2),
-                ALU.add,
+        ident = keep.tile([P, P], F32, name="ident")
+        make_identity(nc, ident[:])
+        z_rows = keep.tile([P, PJ // JB, 2, P, 2], BF16, name="z_rows")
+
+        def add_turned(s):
+            acc = psum.tile([P, PJ // JB, P], F32, name=f"z_t{s}", tag="turn", bufs=2)
+            for jb in range(PJ // JB):
+                js = slice(JB * jb, JB * (jb + 1))
+                nc.tensor.matmul(acc[:, jb, :], lhsT=work[:, s + 1, js], rhs=ident[:], is_transpose=True, start=True, stop=False)
+                nc.tensor.matmul(acc[:, jb, :], lhsT=work[:, s + GAP, js], rhs=ident[:], is_transpose=True, start=False, stop=True)
+            nc.scalar.copy(
+                z_rows[:, :, :, 32 * s : 32 * (s + 1), :],
+                acc[:].rearrange("p b (q u e) -> p b u q e", u=2, e=2),
             )
-            nc.scalar.activation(zb[:, 1, :], zb[:, 0, :], ACT.Abs)
+
+        def turn_back(pair):
+            back = psum.tile([P, 2, 2, JB], F32, name=f"back{pair}", tag="turn", bufs=2)
+            words = z_rows[:].rearrange("p b u q e -> p b u (q e)").bitcast(F32)
+            for b in range(2):
+                for u in range(2):
+                    nc.tensor.transpose(back[:, b, u, :], words[:, 2 * pair + b, u, :], ident[:])
+            return back
 
         y_acc = []
 
@@ -256,44 +288,64 @@ def tile_list_holding_stack_features_kernel(
                     rhs=codes[:, ac].bitcast(FP8X4), rhs_scale=scales[:, ac], start=False, stop=(g == 1 and t == 3),
                 )
 
+        packed = [(w2_raw, w3_raw, ws23)]
         first_stage(0)
-        for a in range(2):
-            w1_q[a, 1] = quantize(round_weight(w1_raw[a, 1], f"w1b{a}1")[:], BANK, f"w1q{a}1")
         first_stage(1)
-        w5_q = []
+        w2_d = keep.tile([P, H], U8, name="w2_d", align_bytes=64)
+        deal(w2_d[:].bitcast(U16), w2_raw[:, H : 2 * H].bitcast(U16), 8, groups=1)
+        w3_d = keep.tile([P, BANK], I32, name="w3_d", align_bytes=64)
+        deal(w3_d[:], w3_raw[:, BANK:H], 4, groups=1)
+        ws23_d = keep.tile([P, BANK], U8, name="ws23_d", tag="ts2", align_bytes=64)
+        deal(ws23_d[:], ws23[:, BANK:H], 16, groups=1)
+        packed.append((w2_d, w3_d, ws23_d))
+        w5_q = [quantize(round_weight(w5_raw[g], f"w5b{g}", dealt=True)[:], N, f"w5q{g}") for g in range(2)]
         for i in range(SLICES + 2):
             if i < SLICES:
                 pick(i)
             if 1 <= i <= SLICES:
                 angles(i - 1)
             if i == 4:
-                w4_d = keep.tile([P, 4 * N], U8, name="w4_d", tag="w3_then_w4", align_bytes=64)
+                w4_d = keep.tile([P, 4 * N], U8, name="w4_d", tag="w1q10_c", align_bytes=64)
                 deal(w4_d[:].bitcast(U16), w4_raw[:].rearrange("p a c -> p (a c)").bitcast(U16), 8)
-                ws4_d = keep.tile([P, 2 * N], U8, name="ws4_d", tag="w2_then_ws4", align_bytes=64)
+                ws4_d = keep.tile([P, 2 * N], U8, name="ws4_d", tag="w1q00_c", align_bytes=64)
                 deal(ws4_d[:], ws4[:], 16)
-            if i + 2 < SLICES:
-                first_stage(i + 2)
-            if i >= 2:
-                products(i - 2)
             if i < SLICES:
                 whole_turns(i)
-            if i == 5:
-                zb0 = big([P, 2, 4 * PJ], BF16, "zb0")
-                join(0, 0, PJ, zb0)
-            if i in (6, 7):
-                w5_q.append(quantize(round_weight(w5_raw[i - 6], f"w5b{i}")[:], N, f"w5q{i}"))
+            if i >= 2:
+                products(i - 2)
+            if i + 2 < SLICES:
+                first_stage(i + 2)
+            if i < SLICES:
+                first_stage_b(i)
+            if i in (5, 6):
+                add_turned(2 * (i - 5))
+                add_turned(2 * (i - 5) + 1)
             if i == 6:
+                zb0 = big([P, 2, 4 * PJ], BF16, "zb0")
+                z_words = zb0[:, 0, :].bitcast(F32).rearrange("p (b j u) -> p b j u", j=JB, u=2)
+                for pair in range(2):
+                    back = turn_back(pair)
+                    nc.scalar.copy(z_words[:, 2 * pair : 2 * pair + 2], back[:].rearrange("p b u j -> p b j u"))
+                nc.scalar.activation(zb0[:, 1, :], zb0[:, 0, :], ACT.Abs)
+            if i == 7:
                 zq0 = quantize(zb0[:].rearrange("p a c -> p (a c)"), 2 * PJ, "zq0")
             if i == 7:
                 for jb in range(PJ // JB):
-                    y_acc.append(psum.tile([P, 4, JB], F32, name=f"y_acc{jb}", tag="bank", bufs=8))
+                    y_acc.append(psum.tile([P, 4, JB], F32, name=f"y_acc{jb}", tag="bank", bufs=6))
                     second_stage(0, jb, zq0, JB * jb, PJ)
 
         zb1 = []
         for jb in range(PJ // JB + 1):
             if jb < PJ // JB:
                 zb1.append(ring.tile([P, 2, 4 * JB], BF16, name=f"zb1{jb}", tag="zb1", bufs=4, align_bytes=64))
-                join(1, JB * jb, JB, zb1[jb])
+                js = slice(JB * jb, JB * (jb + 1))
+                nc.vector.tensor_tensor(
+                    zb1[jb][:, 0, :].rearrange("p (c i t) -> p c t i", i=2, t=4),
+                    work[:, 5:9, js].rearrange("p t (c i) -> p c t i", i=2),
+                    work[:, 4 + GAP : 8 + GAP, js].rearrange("p t (c i) -> p c t i", i=2),
+                    ALU.add,
+                )
+                nc.scalar.activation(zb1[jb][:, 1, :], zb1[jb][:, 0, :], ACT.Abs)
             if jb >= 1:
                 zq1 = quantize(zb1[jb - 1][:].rearrange("p a c -> p (a c)"), 2 * JB, f"zq1{jb - 1}")
                 second_stage(1, jb - 1, zq1, 0, JB)

@@ -4,8 +4,8 @@ from contextlib import ExitStack
 import concourse.mybir as mybir
 from concourse.masks import make_identity
 
-K, K2, K3, H, N, T, S, PJ = 1024, 512, 512, 1024, 512, 2048, 1024, 512
-FLOPS = 2 * H * S * (K + K2 + K3) + 2 * 2 * H * N * PJ
+K, K2, K3, H, N, T, S, PICKS = 1024, 512, 512, 1024, 512, 2048, 1024, 512
+FLOPS = 2 * H * S * (K + K2 + K3) + 2 * 2 * H * N * PICKS
 
 F32 = mybir.dt.float32
 BF16 = mybir.dt.bfloat16
@@ -19,11 +19,20 @@ ALU = mybir.AluOpType
 ACT = mybir.ActivationFunctionType
 
 P = 128
+PACK = 4
+PASS = P * PACK
 BANK = 512
 SLICES = H // P
+BLOCK = 128
+BLOCKS = PICKS // BLOCK
 TWO_PI = 2.0 * math.pi
-JB = 128
 ROUNDER = 1.5 * 2.0**23
+
+LARGE_SLOTS = 7
+STAGE_BANKS = 6
+TURN_BANKS = 2
+CHAIN_SLOTS = 4
+ROW_TILES = 3
 
 
 def tile_list_holding_stack_features_kernel(
@@ -38,336 +47,338 @@ def tile_list_holding_stack_features_kernel(
         ring = ctx.enter_context(tc.tile_pool(name="ring", bufs=2))
         psum = ctx.enter_context(tc.psum_pool(name="psum", bufs=1))
 
-        def big(shape, dtype, name):
-            return ring.tile(shape, dtype, name=name, tag="big", bufs=7, align_bytes=64)
+        def large_tile(shape, dtype, name):
+            return ring.tile(shape, dtype, name=name, tag="large", bufs=LARGE_SLOTS, align_bytes=64)
 
-        def load_list(src, name):
-            t = lists.tile(list(src.shape), U16, name=name)
-            nc.sync.dma_start(t[:], src)
-            return t
+        def load_list(source, name):
+            tile = lists.tile(list(source.shape), U16, name=name)
+            nc.sync.dma_start(tile[:], source)
+            return tile
 
-        def load_table_words(words, a, name):
-            t = big([P, T], I32, name)
-            nc.sync.dma_start(t[:], words[a].rearrange("p t i -> p (t i)").bitcast(I32))
-            return t
+        def load_table_words(words, g, name):
+            tile = large_tile([P, T], I32, name)
+            nc.sync.dma_start(tile[:], words[g].rearrange("p c t -> p (c t)").bitcast(I32))
+            return tile
 
-        def load_weight_rows(w, a, c0, name):
-            t = big([P, 4, BANK], F32, name)
-            nc.sync.dma_start(t[:], w[512 * a : 512 * (a + 1), c0 : c0 + BANK].rearrange("(p j) c -> p j c", j=4))
-            return t
+        def load_weight_rows(weight, g, first_column, name):
+            tile = large_tile([P, PACK, PASS], F32, name)
+            rows = weight[PASS * g : PASS * (g + 1), first_column : first_column + PASS]
+            nc.sync.dma_start(tile[:], rows.rearrange("(p t) c -> p t c", t=PACK))
+            return tile
 
         def zeroed_plane(width, name):
-            t = keep.tile([P, width], U8, name=name, align_bytes=64)
-            nc.vector.memset(t[:].bitcast(I32), 0)
-            return t
+            tile = keep.tile([P, width], U8, name=name, align_bytes=64)
+            nc.vector.memset(tile[:].bitcast(I32), 0)
+            return tile
 
-        def load_scale_rows(queue, plane, scales, first_row, quadrants=(0, 1, 2, 3)):
+        def load_scale_rows(queue, plane, scales, first_row):
             rows = 4 * scales.shape[0]
-            for q in quadrants:
-                p0 = 32 * q + first_row
-                queue.dma_start(plane[p0 : p0 + rows, :].bitcast(I32), scales[:, 4 * q : 4 * q + 4, :].bitcast(I32))
+            for quadrant in range(4):
+                partition = 32 * quadrant + first_row
+                source = scales[:, 4 * quadrant : 4 * quadrant + 4, :]
+                queue.dma_start(plane[partition : partition + rows, :].bitcast(I32), source.bitcast(I32))
 
-        ts1 = zeroed_plane(T, "ts1")
-        ts2 = zeroed_plane(T, "ts2")
-        ts3 = zeroed_plane(T, "ts3")
-        ws23 = zeroed_plane(H, "ws23")
-        ws4 = zeroed_plane(2 * N, "ws4")
-        load_scale_rows(nc.gpsimd, ws23, w2_scales, 0)
-        load_scale_rows(nc.gpsimd, ws23, w3_scales, 4)
+        tab_plane = zeroed_plane(T, "tab_plane")
+        tab2_plane = zeroed_plane(T, "tab2_plane")
+        tab3_plane = zeroed_plane(T, "tab3_plane")
+        w23_plane = zeroed_plane(H, "w23_plane")
+        w4_plane = zeroed_plane(2 * N, "w4_plane")
+        load_scale_rows(nc.gpsimd, w23_plane, w2_scales, 0)
+        load_scale_rows(nc.gpsimd, w23_plane, w3_scales, 4)
 
-        l_offs = load_list(offs, "l_offs")
-        tw10 = load_table_words(tab_words, 0, "tw10")
-        load_scale_rows(nc.sync, ts1, tab_scales, 0)
-        tw11 = load_table_words(tab_words, 1, "tw11")
-        w1_raw = {}
-        w1_raw[0, 0] = load_weight_rows(w1, 0, 0, "w1r00")
-        l_offs3 = load_list(offs3, "l_offs3")
-        w1_raw[1, 0] = load_weight_rows(w1, 1, 0, "w1r10")
-        load_scale_rows(nc.sync, ts3, tab3_scales, 0)
-        w1_raw[0, 1] = load_weight_rows(w1, 0, BANK, "w1r01")
-        tw3 = load_table_words(tab3_words, 0, "tw3")
-        l_offs2 = load_list(offs2, "l_offs2")
-        w1_raw[1, 1] = load_weight_rows(w1, 1, BANK, "w1r11")
-        load_scale_rows(nc.sync, ts2, tab2_scales, 0)
-        w3_raw = keep.tile([P, H], I32, name="w3_raw", align_bytes=64)
-        nc.sync.dma_start(w3_raw[:], w3_words[0].rearrange("p c i -> p (c i)").bitcast(I32))
-        w5_raw = [load_weight_rows(w5, 0, 0, "w5r0")]
-        l_pos1 = load_list(pos1, "l_pos1")
-        w5_raw.append(load_weight_rows(w5, 1, 0, "w5r1"))
-        l_pos3 = load_list(pos3, "l_pos3")
-        tw2 = load_table_words(tab2_words, 0, "tw2")
-        w2_raw = keep.tile([P, 2 * H], U8, name="w2_raw", align_bytes=64)
-        nc.sync.dma_start(w2_raw[:].bitcast(I32), w2_words[0].bitcast(I32))
-        gain_sb = [keep.tile([P, 4], F32, name=f"gain_sb{g}") for g in range(2)]
-        with nc.allow_non_contiguous_dma(reason="one gain value a partition and slice"):
-            nc.sync.dma_start(gain_sb[0][:], gain[0:BANK].rearrange("(t p) -> p t", p=P))
-        nc.sync.dma_start(gain_sb[1][:], gain[BANK:H].rearrange("(p t) -> p t", t=4))
-        l_pos2 = load_list(pos2, "l_pos2")
-        w4_raw = keep.tile([P, 2, 2 * N], U8, name="w4_raw")
-        nc.sync.dma_start(w4_raw[:].bitcast(I32), w4_words.bitcast(I32).rearrange("a p c -> p a c"))
-
-        for q in range(4):
+        idx = load_list(offs, "idx")
+        tab_0 = load_table_words(tab_words, 0, "tab_0")
+        load_scale_rows(nc.sync, tab_plane, tab_scales, 0)
+        tab_1 = load_table_words(tab_words, 1, "tab_1")
+        w1_rows = {}
+        w1_rows[0, 0] = load_weight_rows(w1, 0, 0, "w1_rows_00")
+        idx3 = load_list(offs3, "idx3")
+        w1_rows[1, 0] = load_weight_rows(w1, 1, 0, "w1_rows_10")
+        load_scale_rows(nc.sync, tab3_plane, tab3_scales, 0)
+        w1_rows[0, 1] = load_weight_rows(w1, 0, PASS, "w1_rows_01")
+        tab3 = load_table_words(tab3_words, 0, "tab3")
+        idx2 = load_list(offs2, "idx2")
+        w1_rows[1, 1] = load_weight_rows(w1, 1, PASS, "w1_rows_11")
+        load_scale_rows(nc.sync, tab2_plane, tab2_scales, 0)
+        w3_codes = keep.tile([P, H], I32, name="w3_codes", align_bytes=64)
+        nc.sync.dma_start(w3_codes[:], w3_words[0].rearrange("p c t -> p (c t)").bitcast(I32))
+        w5_rows = [load_weight_rows(w5, 0, 0, "w5_rows_0")]
+        p1 = load_list(pos1, "p1")
+        w5_rows.append(load_weight_rows(w5, 1, 0, "w5_rows_1"))
+        p3 = load_list(pos3, "p3")
+        tab2 = load_table_words(tab2_words, 0, "tab2")
+        w2_codes = keep.tile([P, 2 * H], U8, name="w2_codes", align_bytes=64)
+        nc.sync.dma_start(w2_codes[:].bitcast(I32), w2_words[0].bitcast(I32))
+        gains = [keep.tile([P, PACK], F32, name=f"gains_{g}") for g in range(2)]
+        with nc.allow_non_contiguous_dma(reason="one gain value for each partition and slice"):
+            nc.sync.dma_start(gains[0][:], gain[0:PASS].rearrange("(t p) -> p t", p=P))
+        nc.sync.dma_start(gains[1][:], gain[PASS:H].rearrange("(p t) -> p t", t=PACK))
+        p2 = load_list(pos2, "p2")
+        w4_codes = keep.tile([P, 2, 2 * N], U8, name="w4_codes")
+        nc.sync.dma_start(w4_codes[:].bitcast(I32), w4_words.bitcast(I32).rearrange("g p c -> p g c"))
+        for quadrant in range(4):
             nc.sync.dma_start(
-                ws4[32 * q : 32 * q + 4, :].bitcast(I32).rearrange("p (a c) -> p a c", a=2),
-                w4_scales[:, 4 * q : 4 * q + 4, :].bitcast(I32).rearrange("a r c -> r a c"),
+                w4_plane[32 * quadrant : 32 * quadrant + 4, :].bitcast(I32).rearrange("p (g c) -> p g c", g=2),
+                w4_scales[:, 4 * quadrant : 4 * quadrant + 4, :].bitcast(I32).rearrange("g r c -> r g c"),
             )
 
         def gather_words(table, offsets, name):
-            t = keep.tile([P, S], U32, name=name, align_bytes=64)
-            nc.vector.tensor_copy(t[:], table[:].bitcast(U32).indirect(offsets[:]))
-            return t
+            tile = keep.tile([P, S], U32, name=name, align_bytes=64)
+            nc.vector.tensor_copy(tile[:], table[:].bitcast(U32).indirect(offsets[:]))
+            return tile
 
-        def gather_scales(plane, offsets, name):
-            t = keep.tile([P, S], U8, name=name, align_bytes=64)
-            nc.vector.tensor_copy(t[:], plane[:].indirect(offsets[:]))
-            return t
+        def gather_plane(plane, offsets, name):
+            tile = keep.tile([P, S], U8, name=name, align_bytes=64)
+            nc.vector.tensor_copy(tile[:], plane[:].indirect(offsets[:]))
+            return tile
 
-        def deal(dst, src, run, groups=2):
+        def deal(dealt, source, run, groups):
             nc.vector.tensor_copy(
-                dst.rearrange("p (g t c i) -> p g c t i", g=groups, t=4, i=run),
-                src.rearrange("p (g c i t) -> p g c t i", g=groups, t=4, i=run),
+                dealt.rearrange("p (g t c i) -> p g c t i", g=groups, t=PACK, i=run),
+                source.rearrange("p (g c i t) -> p g c t i", g=groups, t=PACK, i=run),
             )
 
-        def round_weight(raw, name, dealt=False):
-            wb = ring.tile([P, 4 * BANK], BF16, name=name, tag="wb", align_bytes=64)
-            if dealt:
-                nc.scalar.copy(
-                    wb[:].rearrange("p (t q j) -> p q j t", t=4, j=4),
-                    raw[:].rearrange("p j (q t) -> p q j t", t=4),
-                )
-            else:
-                nc.scalar.copy(
-                    wb[:].rearrange("p (c i j) -> p c j i", i=4, j=4),
-                    raw[:].rearrange("p j (c i) -> p c j i", i=4),
-                )
-            return wb
+        def round_weight(rows, name):
+            tile = ring.tile([P, PACK * PASS], BF16, name=name, tag="rounded", align_bytes=64)
+            nc.scalar.copy(
+                tile[:].rearrange("p (c i t) -> p c t i", i=4, t=PACK),
+                rows[:].rearrange("p t (c i) -> p c t i", i=4),
+            )
+            return tile
 
-        def quantize(src, width, name, pool=keep, tag=None, bufs=None):
-            kw = {} if tag is None else {"bufs": bufs}
-            codes = pool.tile([P, width], U32, name=name + "_c", tag=(tag or name) + "_c", align_bytes=64, **kw)
-            scales = pool.tile([P, width], U8, name=name + "_s", tag=(tag or name) + "_s", align_bytes=64, **kw)
-            nc.vector.quantize_mx(out=codes[:].bitcast(FP8X4), scales=scales[:], in_=src)
-            return codes, scales
+        def round_and_deal_weight(rows, name):
+            tile = ring.tile([P, PACK * PASS], BF16, name=name, tag="rounded", align_bytes=64)
+            nc.scalar.copy(
+                tile[:].rearrange("p (u q t) -> p q t u", u=PACK, t=PACK),
+                rows[:].rearrange("p t (q u) -> p q t u", u=PACK),
+            )
+            return tile
 
-        v10 = gather_words(tw10, l_offs, "v10")
-        v11 = gather_words(tw11, l_offs, "v11")
-        vs1 = gather_scales(ts1, l_offs, "vs1")
-        w1_q = {}
-        for a in range(2):
-            w1_q[a, 0] = quantize(round_weight(w1_raw[a, 0], f"w1b{a}0")[:], BANK, f"w1q{a}0")
-        vs3 = gather_scales(ts3, l_offs3, "vs3")
-        vs2 = gather_scales(ts2, l_offs2, "vs2")
-        for a in range(2):
-            w1_q[a, 1] = quantize(round_weight(w1_raw[a, 1], f"w1b{a}1", dealt=True)[:], BANK, f"w1q{a}1")
-        v3 = gather_words(tw3, l_offs3, "v3")
-        v2 = gather_words(tw2, l_offs2, "v2")
-        gain_turn = keep.tile([P, SLICES], F32, name="gain_turn")
+        def quantize(values, width, name):
+            codes = keep.tile([P, width], U32, name=name + "_codes", align_bytes=64)
+            plane = keep.tile([P, width], U8, name=name + "_plane", align_bytes=64)
+            nc.vector.quantize_mx(out=codes[:].bitcast(FP8X4), scales=plane[:], in_=values)
+            return codes, plane
+
+        v_passes = [gather_words(tab_0, idx, "v_0"), gather_words(tab_1, idx, "v_1")]
+        v_plane = gather_plane(tab_plane, idx, "v_plane")
+        w1_mx = {}
+        for k_pass in range(2):
+            w1_mx[k_pass, 0] = quantize(round_weight(w1_rows[k_pass, 0], f"w1_bf_{k_pass}0")[:], PASS, f"w1_{k_pass}0")
+        v3_plane = gather_plane(tab3_plane, idx3, "v3_plane")
+        v2_plane = gather_plane(tab2_plane, idx2, "v2_plane")
+        for k_pass in range(2):
+            rounded = round_and_deal_weight(w1_rows[k_pass, 1], f"w1_bf_{k_pass}1")
+            w1_mx[k_pass, 1] = quantize(rounded[:], PASS, f"w1_{k_pass}1")
+        v3 = gather_words(tab3, idx3, "v3")
+        v2 = gather_words(tab2, idx2, "v2")
+        turn_gains = keep.tile([P, SLICES], F32, name="turn_gains")
         for g in range(2):
-            nc.scalar.activation(gain_turn[:, 4 * g : 4 * g + 4], gain_sb[g][:], ACT.Copy, scale=TWO_PI)
+            nc.scalar.activation(turn_gains[:, PACK * g : PACK * (g + 1)], gains[g][:], ACT.Copy, scale=TWO_PI)
 
-        work = keep.tile([P, 2 * SLICES + 1, PJ], F32, name="work")
-        GAP = SLICES + 1
-        windows = {}
-        windows_b = {}
-        trig = {}
-        whole = {}
+        A_ROW = SLICES + 1
+        work = keep.tile([P, A_ROW + SLICES, PICKS], F32, name="work")
+        a_rows, b_rows, d_rows, whole, trig = {}, {}, {}, {}, {}
 
-        def bank(name):
-            return psum.tile([P, BANK], F32, name=name, tag="bank", bufs=6)
+        def stage_bank(shape, name):
+            return psum.tile(shape, F32, name=name, tag="stage", bufs=STAGE_BANKS)
 
-        def slot_tile(shape, dtype, name, slot):
-            return ring.tile(shape, dtype, name=name, tag=f"slot{slot % 3}", bufs=1)
+        def chain_tile(shape, dtype, name, slot):
+            return ring.tile(shape, dtype, name=name, tag=f"chain_{slot % CHAIN_SLOTS}", bufs=1)
 
-        def first_stage(s):
-            g, t = divmod(s, 4)
+        def multiply_a_d(s):
+            g, t = divmod(s, PACK)
             cols = slice(P * t, P * (t + 1))
-            w2_g, w3_g, ws23_g = packed[g]
-            win_a = ring.tile([P, S], F32, name=f"win_a{s}", tag="win_a", bufs=3)
-            win_d = slot_tile([P, S], F32, f"win_d{s}", s)
-            for h in range(2):
-                m = slice(BANK * h, BANK * (h + 1))
-                acc = bank(f"a{s}{h}")
-                for a, v in enumerate((v10, v11)):
-                    codes, scales = w1_q[a, g]
+            a_rows[s] = ring.tile([P, S], F32, name=f"a_{s}", tag="a", bufs=ROW_TILES)
+            d_rows[s] = chain_tile([P, S], F32, f"d_{s}", s)
+            for half in range(S // BANK):
+                m = slice(BANK * half, BANK * (half + 1))
+                acc = stage_bank([P, BANK], f"a_acc_{s}_{half}")
+                for k_pass in range(2):
+                    codes, plane = w1_mx[k_pass, g]
                     nc.tensor.matmul_mx(
-                        acc[:], lhsT=codes[:, cols].bitcast(FP8X4), lhsT_scale=scales[:, cols],
-                        rhs=v[:, m].bitcast(FP8X4), rhs_scale=vs1[4 * a : P, m], start=(a == 0), stop=(a == 1),
+                        acc[:], lhsT=codes[:, cols].bitcast(FP8X4), lhsT_scale=plane[:, cols],
+                        rhs=v_passes[k_pass][:, m].bitcast(FP8X4), rhs_scale=v_plane[4 * k_pass : P, m],
+                        start=(k_pass == 0), stop=(k_pass == 1),
                     )
-                nc.scalar.activation(win_a[:, m], acc[:], ACT.Copy, scale=1.0 / TWO_PI)
-            for h in range(2):
-                m = slice(BANK * h, BANK * (h + 1))
-                acc = bank(f"d{s}{h}")
+                nc.scalar.activation(a_rows[s][:, m], acc[:], ACT.Copy, scale=1.0 / TWO_PI)
+            for half in range(S // BANK):
+                m = slice(BANK * half, BANK * (half + 1))
+                acc = stage_bank([P, BANK], f"d_acc_{s}_{half}")
                 nc.tensor.matmul_mx(
-                    acc[:], lhsT=w3_g[:, cols].bitcast(FP8X4), lhsT_scale=ws23_g[4:P, cols],
-                    rhs=v3[:, m].bitcast(FP8X4), rhs_scale=vs3[:, m], start=True, stop=True,
+                    acc[:], lhsT=w3_by_pass[g][:, cols].bitcast(FP8X4), lhsT_scale=w23_plane_by_pass[g][4:P, cols],
+                    rhs=v3[:, m].bitcast(FP8X4), rhs_scale=v3_plane[:, m], start=True, stop=True,
                 )
-                nc.scalar.activation(win_d[:, m], acc[:], ACT.Copy, scale=1.0 / TWO_PI, bias=0.25)
-            windows[s] = (win_a, win_d)
+                nc.scalar.activation(d_rows[s][:, m], acc[:], ACT.Copy, scale=1.0 / TWO_PI, bias=0.25)
 
-        def first_stage_b(s):
-            g, t = divmod(s, 4)
-            cols = slice(P * t, P * (t + 1))
-            w2_g, w3_g, ws23_g = packed[g]
-            win_b = ring.tile([P, S], F32, name=f"win_b{s}", tag="win_b", bufs=3)
-            for h in range(2):
-                m = slice(BANK * h, BANK * (h + 1))
-                acc = bank(f"b{s}{h}")
+        def multiply_b(s):
+            g, t = divmod(s, PACK)
+            b_rows[s] = ring.tile([P, S], F32, name=f"b_{s}", tag="b", bufs=ROW_TILES)
+            for half in range(S // BANK):
+                m = slice(BANK * half, BANK * (half + 1))
+                acc = stage_bank([P, BANK], f"b_acc_{s}_{half}")
                 nc.tensor.matmul_mx(
-                    acc[:], lhsT=w2_g[:, 2 * P * t : 2 * P * (t + 1)].bitcast(FP4X4), lhsT_scale=ws23_g[:, cols],
-                    rhs=v2[:, m].bitcast(FP8X4), rhs_scale=vs2[:, m], start=True, stop=True,
+                    acc[:], lhsT=w2_by_pass[g][:, 2 * P * t : 2 * P * (t + 1)].bitcast(FP4X4),
+                    lhsT_scale=w23_plane_by_pass[g][:, P * t : P * (t + 1)],
+                    rhs=v2[:, m].bitcast(FP8X4), rhs_scale=v2_plane[:, m], start=True, stop=True,
                 )
-                nc.scalar.activation(win_b[:, m], acc[:], ACT.Copy, scale=gain_sb[g][:, t : t + 1])
-            windows_b[s] = win_b
+                nc.scalar.activation(b_rows[s][:, m], acc[:], ACT.Copy, scale=gains[g][:, t : t + 1])
 
-        def pick(s):
-            win_a, win_d = windows[s]
-            nc.vector.tensor_copy(work[:, s + GAP, :], win_a[:].indirect(l_pos1[:]))
-            nc.vector.tensor_copy(work[:, s, :], win_d[:].indirect(l_pos3[:]))
+        def pick_angles(s):
+            nc.vector.tensor_copy(work[:, A_ROW + s, :], a_rows[s][:].indirect(p1[:]))
+            nc.vector.tensor_copy(work[:, s, :], d_rows[s][:].indirect(p3[:]))
 
-        def whole_turns(s):
-            whole[s] = ring.tile([P, 2, PJ], I32, name=f"whole{s}", tag="whole")
-            turns = work[:, s : s + GAP + 1 : GAP, :]
-            if s < 6:
-                nc.scalar.activation(whole[s][:].bitcast(U32), turns, ACT.Copy, bias=ROUNDER)
+        def picked_turns(s):
+            return work[:, s : A_ROW + s + 1 : A_ROW, :]
+
+        def round_turns(s):
+            whole[s] = chain_tile([P, 2, PICKS], I32, f"whole_{s}", s - 1)
+            if s + 1 < SLICES:
+                nc.gpsimd.tensor_scalar(whole[s][:], picked_turns(s), 1.0, ROUNDER, ALU.mult, ALU.add)
             else:
-                nc.vector.tensor_scalar(whole[s][:], turns, ROUNDER, None, ALU.add)
+                nc.scalar.activation(whole[s][:].bitcast(U32), picked_turns(s), ACT.Copy, bias=ROUNDER)
 
-        def angles(s):
-            frac = slot_tile([P, 2, PJ], F32, f"frac{s}", s + 1)
-            nc.vector.scalar_tensor_tensor(
-                frac[:], whole[s][:], ROUNDER, work[:, s : s + GAP + 1 : GAP, :], ALU.subtract, ALU.subtract
-            )
-            nc.scalar.activation(frac[:], frac[:], ACT.Sin, scale=-TWO_PI)
-            trig[s] = frac
+        def sines(s):
+            trig[s] = chain_tile([P, 2, PICKS], F32, f"trig_{s}", s + 1)
+            nc.vector.scalar_tensor_tensor(trig[s][:], whole[s][:], ROUNDER, picked_turns(s), ALU.subtract, ALU.subtract)
+            nc.scalar.activation(trig[s][:], trig[s][:], ACT.Sin, scale=-TWO_PI)
 
-        def products(s):
-            win_b = windows_b[s]
-            nc.vector.tensor_tensor(work[:, s + 1, :], win_b[:].indirect(l_pos2[:]), trig[s][:, 1, :], ALU.mult)
-            nc.vector.scalar_tensor_tensor(
-                work[:, s + GAP, :], trig[s][:, 0, :], gain_turn[:, s : s + 1], work[:, s + GAP, :], ALU.mult, ALU.mult
-            )
+        def terms(s):
+            picked_a = work[:, A_ROW + s, :]
+            nc.vector.scalar_tensor_tensor(picked_a, trig[s][:, 0, :], turn_gains[:, s : s + 1], picked_a, ALU.mult, ALU.mult)
+            nc.vector.tensor_tensor(work[:, s + 1, :], b_rows[s][:].indirect(p2[:]), trig[s][:, 1, :], ALU.mult)
 
-        ident = keep.tile([P, P], F32, name="ident")
-        make_identity(nc, ident[:])
-        z_rows = keep.tile([P, PJ // JB, 2, P, 2], BF16, name="z_rows")
+        identity = keep.tile([P, P], F32, name="identity")
+        make_identity(nc, identity[:])
+        z_turned = keep.tile([P, BLOCKS, 2, P, 2], BF16, name="z_turned")
 
         def add_turned(s):
-            acc = psum.tile([P, PJ // JB, P], F32, name=f"z_t{s}", tag="turn", bufs=2)
-            for jb in range(PJ // JB):
-                js = slice(JB * jb, JB * (jb + 1))
-                nc.tensor.matmul(acc[:, jb, :], lhsT=work[:, s + 1, js], rhs=ident[:], is_transpose=True, start=True, stop=False)
-                nc.tensor.matmul(acc[:, jb, :], lhsT=work[:, s + GAP, js], rhs=ident[:], is_transpose=True, start=False, stop=True)
+            acc = psum.tile([P, BLOCKS, P], F32, name=f"z_sum_{s}", tag="turn", bufs=TURN_BANKS)
+            for block in range(BLOCKS):
+                js = slice(BLOCK * block, BLOCK * (block + 1))
+                for row, opens in ((s + 1, True), (A_ROW + s, False)):
+                    nc.tensor.matmul(
+                        acc[:, block, :], lhsT=work[:, row, js], rhs=identity[:], is_transpose=True, start=opens, stop=not opens
+                    )
             nc.scalar.copy(
-                z_rows[:, :, :, 32 * s : 32 * (s + 1), :],
-                acc[:].rearrange("p b (q u e) -> p b u q e", u=2, e=2),
+                z_turned[:, :, :, 32 * s : 32 * (s + 1), :],
+                acc[:].rearrange("j b (q u e) -> j b u q e", u=2, e=2),
             )
 
-        def turn_back(pair):
-            back = psum.tile([P, 2, 2, JB], F32, name=f"back{pair}", tag="turn", bufs=2)
-            words = z_rows[:].rearrange("p b u q e -> p b u (q e)").bitcast(F32)
-            for b in range(2):
-                for u in range(2):
-                    nc.tensor.transpose(back[:, b, u, :], words[:, 2 * pair + b, u, :], ident[:])
-            return back
+        def turn_back(z_pass):
+            turned_pairs = z_turned[:].rearrange("j b u q e -> j b u (q e)").bitcast(F32)
+            pairs = z_pass.bitcast(F32).rearrange("q (b j u) -> q b j u", j=BLOCK, u=2)
+            for block in range(0, BLOCKS, 2):
+                back = psum.tile([P, 2, 2, BLOCK], F32, name=f"z_back_{block}", tag="turn", bufs=TURN_BANKS)
+                for b in range(2):
+                    for u in range(2):
+                        nc.tensor.transpose(back[:, b, u, :], turned_pairs[:, block + b, u, :], identity[:])
+                nc.scalar.copy(pairs[:, block : block + 2], back[:].rearrange("q b u j -> q b j u"))
 
         y_acc = []
 
-        def second_stage(g, jb, zq, c0, width):
-            codes, scales = zq
-            for t in range(4):
+        def multiply_y(g, block, z_mx, first_column, width):
+            codes, plane = z_mx
+            z_cols = slice(first_column, first_column + BLOCK)
+            abs_cols = slice(width + first_column, width + first_column + BLOCK)
+            w5_codes, w5_plane = w5_mx[g]
+            for t in range(PACK):
                 cols = slice(P * t, P * (t + 1))
-                wc = N * g + P * t
-                zc = slice(c0, c0 + JB)
-                ac = slice(width + c0, width + c0 + JB)
+                w4_column = N * g + P * t
                 nc.tensor.matmul_mx(
-                    y_acc[jb][:, t, :], lhsT=w4_d[:, 2 * wc : 2 * wc + 2 * P].bitcast(FP4X4), lhsT_scale=ws4_d[:, wc : wc + P],
-                    rhs=codes[:, zc].bitcast(FP8X4), rhs_scale=scales[:, zc], start=(g == 0 and t == 0), stop=False,
+                    y_acc[block][:, t, :], lhsT=w4_dealt[:, 2 * w4_column : 2 * (w4_column + P)].bitcast(FP4X4),
+                    lhsT_scale=w4_plane_dealt[:, w4_column : w4_column + P],
+                    rhs=codes[:, z_cols].bitcast(FP8X4), rhs_scale=plane[:, z_cols],
+                    start=(g == 0 and t == 0), stop=False,
                 )
                 nc.tensor.matmul_mx(
-                    y_acc[jb][:, t, :], lhsT=w5_q[g][0][:, cols].bitcast(FP8X4), lhsT_scale=w5_q[g][1][:, cols],
-                    rhs=codes[:, ac].bitcast(FP8X4), rhs_scale=scales[:, ac], start=False, stop=(g == 1 and t == 3),
+                    y_acc[block][:, t, :], lhsT=w5_codes[:, cols].bitcast(FP8X4), lhsT_scale=w5_plane[:, cols],
+                    rhs=codes[:, abs_cols].bitcast(FP8X4), rhs_scale=plane[:, abs_cols],
+                    start=False, stop=(g == 1 and t == PACK - 1),
                 )
 
-        packed = [(w2_raw, w3_raw, ws23)]
-        first_stage(0)
-        first_stage(1)
-        w2_d = keep.tile([P, H], U8, name="w2_d", align_bytes=64)
-        deal(w2_d[:].bitcast(U16), w2_raw[:, H : 2 * H].bitcast(U16), 8, groups=1)
-        w3_d = keep.tile([P, BANK], I32, name="w3_d", align_bytes=64)
-        deal(w3_d[:], w3_raw[:, BANK:H], 4, groups=1)
-        ws23_d = keep.tile([P, BANK], U8, name="ws23_d", tag="ts2", align_bytes=64)
-        deal(ws23_d[:], ws23[:, BANK:H], 16, groups=1)
-        packed.append((w2_d, w3_d, ws23_d))
-        w5_q = [quantize(round_weight(w5_raw[g], f"w5b{g}", dealt=True)[:], N, f"w5q{g}") for g in range(2)]
+        w2_by_pass, w3_by_pass, w23_plane_by_pass = [w2_codes], [w3_codes], [w23_plane]
+        multiply_a_d(0)
+        multiply_a_d(1)
+        w2_dealt = keep.tile([P, 2 * PASS], U8, name="w2_dealt", align_bytes=64)
+        deal(w2_dealt[:].bitcast(U16), w2_codes[:, 2 * PASS : 2 * H].bitcast(U16), 8, 1)
+        w3_dealt = keep.tile([P, PASS], I32, name="w3_dealt", align_bytes=64)
+        deal(w3_dealt[:], w3_codes[:, PASS:H], 4, 1)
+        w23_plane_dealt = keep.tile([P, PASS], U8, name="w23_plane_dealt", tag="tab2_plane", align_bytes=64)
+        deal(w23_plane_dealt[:], w23_plane[:, PASS:H], 16, 1)
+        w2_by_pass.append(w2_dealt)
+        w3_by_pass.append(w3_dealt)
+        w23_plane_by_pass.append(w23_plane_dealt)
+        w5_mx = [quantize(round_and_deal_weight(w5_rows[g], f"w5_bf_{g}")[:], N, f"w5_{g}") for g in range(2)]
+
+        PASS_0_TERMS_DONE = PACK + 1
         for i in range(SLICES + 2):
             if i < SLICES:
-                pick(i)
+                pick_angles(i)
             if 1 <= i <= SLICES:
-                angles(i - 1)
-            if i == 4:
-                w4_d = keep.tile([P, 4 * N], U8, name="w4_d", tag="w1q10_c", align_bytes=64)
-                deal(w4_d[:].bitcast(U16), w4_raw[:].rearrange("p a c -> p (a c)").bitcast(U16), 8)
-                ws4_d = keep.tile([P, 2 * N], U8, name="ws4_d", tag="w1q00_c", align_bytes=64)
-                deal(ws4_d[:], ws4[:], 16)
-            if i < SLICES:
-                whole_turns(i)
-            if i >= 2:
-                products(i - 2)
+                sines(i - 1)
+            if i == PACK:
+                w4_dealt = keep.tile([P, 4 * N], U8, name="w4_dealt", tag="w1_10_codes", align_bytes=64)
+                deal(w4_dealt[:].bitcast(U16), w4_codes[:].rearrange("p g c -> p (g c)").bitcast(U16), 8, 2)
+                w4_plane_dealt = keep.tile([P, 2 * N], U8, name="w4_plane_dealt", tag="w1_00_codes", align_bytes=64)
+                deal(w4_plane_dealt[:], w4_plane[:], 16, 2)
             if i + 2 < SLICES:
-                first_stage(i + 2)
+                multiply_a_d(i + 2)
+            if i >= 2:
+                terms(i - 2)
             if i < SLICES:
-                first_stage_b(i)
-            if i in (5, 6):
-                add_turned(2 * (i - 5))
-                add_turned(2 * (i - 5) + 1)
-            if i == 6:
-                zb0 = big([P, 2, 4 * PJ], BF16, "zb0")
-                z_words = zb0[:, 0, :].bitcast(F32).rearrange("p (b j u) -> p b j u", j=JB, u=2)
-                for pair in range(2):
-                    back = turn_back(pair)
-                    nc.scalar.copy(z_words[:, 2 * pair : 2 * pair + 2], back[:].rearrange("p b u j -> p b j u"))
-                nc.scalar.activation(zb0[:, 1, :], zb0[:, 0, :], ACT.Abs)
-            if i == 7:
-                zq0 = quantize(zb0[:].rearrange("p a c -> p (a c)"), 2 * PJ, "zq0")
-            if i == 7:
-                for jb in range(PJ // JB):
-                    y_acc.append(psum.tile([P, 4, JB], F32, name=f"y_acc{jb}", tag="bank", bufs=6))
-                    second_stage(0, jb, zq0, JB * jb, PJ)
+                round_turns(i)
+                multiply_b(i)
+            if 2 <= i <= PASS_0_TERMS_DONE:
+                add_turned(i - 2)
+            if i == PASS_0_TERMS_DONE:
+                z_0 = large_tile([P, 2, PACK * PICKS], BF16, "z_0")
+                turn_back(z_0[:, 0, :])
+                nc.scalar.activation(z_0[:, 1, :], z_0[:, 0, :], ACT.Abs)
+            if i == PASS_0_TERMS_DONE + 1:
+                z_0_mx = quantize(z_0[:].rearrange("p a c -> p (a c)"), 2 * PICKS, "z_0")
+            if i == SLICES - 1:
+                for block in range(BLOCKS):
+                    y_acc.append(stage_bank([P, PACK, BLOCK], f"y_acc_{block}"))
+                    multiply_y(0, block, z_0_mx, BLOCK * block, PICKS)
 
-        zb1 = []
-        for jb in range(PJ // JB + 1):
-            if jb < PJ // JB:
-                zb1.append(ring.tile([P, 2, 4 * JB], BF16, name=f"zb1{jb}", tag="zb1", bufs=4, align_bytes=64))
-                js = slice(JB * jb, JB * (jb + 1))
+        z_1 = []
+        for block in range(BLOCKS + 1):
+            if block < BLOCKS:
+                z_1.append(ring.tile([P, 2, PACK * BLOCK], BF16, name=f"z_1_{block}", tag="z_1", bufs=BLOCKS, align_bytes=64))
+                js = slice(BLOCK * block, BLOCK * (block + 1))
                 nc.vector.tensor_tensor(
-                    zb1[jb][:, 0, :].rearrange("p (c i t) -> p c t i", i=2, t=4),
-                    work[:, 5:9, js].rearrange("p t (c i) -> p c t i", i=2),
-                    work[:, 4 + GAP : 8 + GAP, js].rearrange("p t (c i) -> p c t i", i=2),
+                    z_1[block][:, 0, :].rearrange("p (c i t) -> p c t i", i=2, t=PACK),
+                    work[:, PACK + 1 : SLICES + 1, js].rearrange("p t (c i) -> p c t i", i=2),
+                    work[:, A_ROW + PACK : A_ROW + SLICES, js].rearrange("p t (c i) -> p c t i", i=2),
                     ALU.add,
                 )
-                nc.scalar.activation(zb1[jb][:, 1, :], zb1[jb][:, 0, :], ACT.Abs)
-            if jb >= 1:
-                zq1 = quantize(zb1[jb - 1][:].rearrange("p a c -> p (a c)"), 2 * JB, f"zq1{jb - 1}")
-                second_stage(1, jb - 1, zq1, 0, JB)
+                nc.scalar.activation(z_1[block][:, 1, :], z_1[block][:, 0, :], ACT.Abs)
+            if block >= 1:
+                z_1_mx = quantize(z_1[block - 1][:].rearrange("p a c -> p (a c)"), 2 * BLOCK, f"z_1_{block - 1}")
+                multiply_y(1, block - 1, z_1_mx, 0, BLOCK)
 
-        y_codes = keep.tile([P, PJ], U32, name="y_codes", align_bytes=64)
-        y_scales = keep.tile([P, PJ], U8, name="y_scales", align_bytes=64)
-        out_rows = out_0.rearrange("(p t) j -> p t j", t=4)
-        out_words = out_1[0].rearrange("p m t -> p (m t)").bitcast(I32)
-        for jb in range(PJ // JB):
-            js = slice(JB * jb, JB * (jb + 1))
-            y_sb = ring.tile([P, 4, JB], F32, name=f"y_sb{jb}", tag="y_sb", bufs=4)
-            nc.scalar.copy(y_sb[:], y_acc[jb][:])
-            nc.sync.dma_start(out_rows[:, :, js], y_sb[:])
-            yb = ring.tile([P, 4 * JB], BF16, name=f"yb{jb}", tag="yb", align_bytes=64)
+        y_codes = keep.tile([P, PICKS], U32, name="y_codes", align_bytes=64)
+        y_plane = keep.tile([P, PICKS], U8, name="y_plane", align_bytes=64)
+        out_rows = out_0.rearrange("(p t) j -> p t j", t=PACK)
+        out_words = out_1[0].rearrange("p j t -> p (j t)").bitcast(I32)
+        for block in range(BLOCKS):
+            js = slice(BLOCK * block, BLOCK * (block + 1))
+            y = ring.tile([P, PACK, BLOCK], F32, name=f"y_{block}", tag="y", bufs=BLOCKS)
+            nc.scalar.copy(y[:], y_acc[block][:])
+            nc.sync.dma_start(out_rows[:, :, js], y[:])
+            y_bf = ring.tile([P, PACK * BLOCK], BF16, name=f"y_bf_{block}", tag="y_bf", align_bytes=64)
             nc.vector.tensor_copy(
-                yb[:].rearrange("p (c i t) -> p c t i", i=2, t=4),
-                y_sb[:].rearrange("p t (c i) -> p c t i", i=2),
+                y_bf[:].rearrange("p (c i t) -> p c t i", i=2, t=PACK),
+                y[:].rearrange("p t (c i) -> p c t i", i=2),
             )
-            nc.vector.quantize_mx(out=y_codes[:, js].bitcast(FP8X4), scales=y_scales[:, js], in_=yb[:])
-            if jb >= 2:
-                done = slice(0, 3 * JB) if jb == 2 else js
+            nc.vector.quantize_mx(out=y_codes[:, js].bitcast(FP8X4), scales=y_plane[:, js], in_=y_bf[:])
+            if block >= BLOCKS - 2:
+                done = js if block == BLOCKS - 1 else slice(0, js.stop)
                 nc.scalar.dma_start(out_words[:, done], y_codes[:, done].bitcast(I32))
-        for q in range(4):
-            queue = nc.sync if q % 2 == 0 else nc.scalar
-            queue.dma_start(out_2[0, 4 * q : 4 * q + 4, :].bitcast(I32), y_scales[32 * q : 32 * q + 4, :].bitcast(I32))
+        for quadrant in range(4):
+            queue = nc.sync if quadrant % 2 == 0 else nc.scalar
+            queue.dma_start(
+                out_2[0, 4 * quadrant : 4 * quadrant + 4, :].bitcast(I32),
+                y_plane[32 * quadrant : 32 * quadrant + 4, :].bitcast(I32),
+            )

import math
from contextlib import ExitStack

import concourse.mybir as mybir
from concourse.masks import make_identity

K, K2, K3, H, N, T, S, PICKS = 1024, 512, 512, 1024, 512, 2048, 1024, 512
FLOPS = 2 * H * S * (K + K2 + K3) + 2 * 2 * H * N * PICKS

F32 = mybir.dt.float32
BF16 = mybir.dt.bfloat16
I32 = mybir.dt.int32
U32 = mybir.dt.uint32
U16 = mybir.dt.uint16
U8 = mybir.dt.uint8
FP8X4 = mybir.dt.float8_e4m3fn_x4
FP4X4 = mybir.dt.float4_e2m1fn_x4
ALU = mybir.AluOpType
ACT = mybir.ActivationFunctionType

P = 128
PACK = 4
PASS = P * PACK
BANK = 512
SLICES = H // P
BLOCK = 128
BLOCKS = PICKS // BLOCK
TWO_PI = 2.0 * math.pi
ROUNDER = 1.5 * 2.0**23

LARGE_SLOTS = 7
STAGE_BANKS = 6
TURN_BANKS = 2
CHAIN_SLOTS = 4
ROW_TILES = 3


def tile_list_holding_stack_features_kernel(
    tc, tab_words, tab_scales, tab2_words, tab2_scales, tab3_words, tab3_scales,
    offs, offs2, offs3, pos1, pos2, pos3, w1, w2_words, w2_scales, w3_words, w3_scales,
    gain, w4_words, w4_scales, w5, out_0, out_1, out_2,
):
    nc = tc.nc
    with ExitStack() as ctx:
        lists = ctx.enter_context(tc.tile_pool(name="lists", bufs=1))
        keep = ctx.enter_context(tc.tile_pool(name="keep", bufs=1))
        ring = ctx.enter_context(tc.tile_pool(name="ring", bufs=2))
        psum = ctx.enter_context(tc.psum_pool(name="psum", bufs=1))

        def large_tile(shape, dtype, name):
            return ring.tile(shape, dtype, name=name, tag="large", bufs=LARGE_SLOTS, align_bytes=64)

        def load_list(source, name):
            tile = lists.tile(list(source.shape), U16, name=name)
            nc.sync.dma_start(tile[:], source)
            return tile

        def load_table_words(words, g, name):
            tile = large_tile([P, T], I32, name)
            nc.sync.dma_start(tile[:], words[g].rearrange("p c t -> p (c t)").bitcast(I32))
            return tile

        def load_weight_rows(weight, g, first_column, name):
            tile = large_tile([P, PACK, PASS], F32, name)
            rows = weight[PASS * g : PASS * (g + 1), first_column : first_column + PASS]
            nc.sync.dma_start(tile[:], rows.rearrange("(p t) c -> p t c", t=PACK))
            return tile

        def zeroed_plane(width, name):
            tile = keep.tile([P, width], U8, name=name, align_bytes=64)
            nc.vector.memset(tile[:].bitcast(I32), 0)
            return tile

        def load_scale_rows(queue, plane, scales, first_row):
            rows = 4 * scales.shape[0]
            for quadrant in range(4):
                partition = 32 * quadrant + first_row
                source = scales[:, 4 * quadrant : 4 * quadrant + 4, :]
                queue.dma_start(plane[partition : partition + rows, :].bitcast(I32), source.bitcast(I32))

        tab_plane = zeroed_plane(T, "tab_plane")
        tab2_plane = zeroed_plane(T, "tab2_plane")
        tab3_plane = zeroed_plane(T, "tab3_plane")
        w23_plane = zeroed_plane(H, "w23_plane")
        w4_plane = zeroed_plane(2 * N, "w4_plane")
        load_scale_rows(nc.gpsimd, w23_plane, w2_scales, 0)
        load_scale_rows(nc.gpsimd, w23_plane, w3_scales, 4)

        idx = load_list(offs, "idx")
        tab_0 = load_table_words(tab_words, 0, "tab_0")
        load_scale_rows(nc.sync, tab_plane, tab_scales, 0)
        tab_1 = load_table_words(tab_words, 1, "tab_1")
        w1_rows = {}
        w1_rows[0, 0] = load_weight_rows(w1, 0, 0, "w1_rows_00")
        idx3 = load_list(offs3, "idx3")
        w1_rows[1, 0] = load_weight_rows(w1, 1, 0, "w1_rows_10")
        load_scale_rows(nc.sync, tab3_plane, tab3_scales, 0)
        w1_rows[0, 1] = load_weight_rows(w1, 0, PASS, "w1_rows_01")
        tab3 = load_table_words(tab3_words, 0, "tab3")
        idx2 = load_list(offs2, "idx2")
        w1_rows[1, 1] = load_weight_rows(w1, 1, PASS, "w1_rows_11")
        load_scale_rows(nc.sync, tab2_plane, tab2_scales, 0)
        w3_codes = keep.tile([P, H], I32, name="w3_codes", align_bytes=64)
        nc.sync.dma_start(w3_codes[:], w3_words[0].rearrange("p c t -> p (c t)").bitcast(I32))
        w5_rows = [load_weight_rows(w5, 0, 0, "w5_rows_0")]
        p1 = load_list(pos1, "p1")
        w5_rows.append(load_weight_rows(w5, 1, 0, "w5_rows_1"))
        p3 = load_list(pos3, "p3")
        tab2 = load_table_words(tab2_words, 0, "tab2")
        w2_codes = keep.tile([P, 2 * H], U8, name="w2_codes", align_bytes=64)
        nc.sync.dma_start(w2_codes[:].bitcast(I32), w2_words[0].bitcast(I32))
        gains = [keep.tile([P, PACK], F32, name=f"gains_{g}") for g in range(2)]
        with nc.allow_non_contiguous_dma(reason="one gain value for each partition and slice"):
            nc.sync.dma_start(gains[0][:], gain[0:PASS].rearrange("(t p) -> p t", p=P))
        nc.sync.dma_start(gains[1][:], gain[PASS:H].rearrange("(p t) -> p t", t=PACK))
        p2 = load_list(pos2, "p2")
        w4_codes = keep.tile([P, 2, 2 * N], U8, name="w4_codes")
        nc.sync.dma_start(w4_codes[:].bitcast(I32), w4_words.bitcast(I32).rearrange("g p c -> p g c"))
        for quadrant in range(4):
            nc.sync.dma_start(
                w4_plane[32 * quadrant : 32 * quadrant + 4, :].bitcast(I32).rearrange("p (g c) -> p g c", g=2),
                w4_scales[:, 4 * quadrant : 4 * quadrant + 4, :].bitcast(I32).rearrange("g r c -> r g c"),
            )

        def gather_words(table, offsets, name):
            tile = keep.tile([P, S], U32, name=name, align_bytes=64)
            nc.vector.tensor_copy(tile[:], table[:].bitcast(U32).indirect(offsets[:]))
            return tile

        def gather_plane(plane, offsets, name):
            tile = keep.tile([P, S], U8, name=name, align_bytes=64)
            nc.vector.tensor_copy(tile[:], plane[:].indirect(offsets[:]))
            return tile

        def deal(dealt, source, run, groups):
            nc.vector.tensor_copy(
                dealt.rearrange("p (g t c i) -> p g c t i", g=groups, t=PACK, i=run),
                source.rearrange("p (g c i t) -> p g c t i", g=groups, t=PACK, i=run),
            )

        def round_weight(rows, name):
            tile = ring.tile([P, PACK * PASS], BF16, name=name, tag="rounded", align_bytes=64)
            nc.scalar.copy(
                tile[:].rearrange("p (c i t) -> p c t i", i=4, t=PACK),
                rows[:].rearrange("p t (c i) -> p c t i", i=4),
            )
            return tile

        def round_and_deal_weight(rows, name):
            tile = ring.tile([P, PACK * PASS], BF16, name=name, tag="rounded", align_bytes=64)
            nc.scalar.copy(
                tile[:].rearrange("p (u q t) -> p q t u", u=PACK, t=PACK),
                rows[:].rearrange("p t (q u) -> p q t u", u=PACK),
            )
            return tile

        def quantize(values, width, name):
            codes = keep.tile([P, width], U32, name=name + "_codes", align_bytes=64)
            plane = keep.tile([P, width], U8, name=name + "_plane", align_bytes=64)
            nc.vector.quantize_mx(out=codes[:].bitcast(FP8X4), scales=plane[:], in_=values)
            return codes, plane

        v_passes = [gather_words(tab_0, idx, "v_0"), gather_words(tab_1, idx, "v_1")]
        v_plane = gather_plane(tab_plane, idx, "v_plane")
        w1_mx = {}
        for k_pass in range(2):
            w1_mx[k_pass, 0] = quantize(round_weight(w1_rows[k_pass, 0], f"w1_bf_{k_pass}0")[:], PASS, f"w1_{k_pass}0")
        v3_plane = gather_plane(tab3_plane, idx3, "v3_plane")
        v2_plane = gather_plane(tab2_plane, idx2, "v2_plane")
        for k_pass in range(2):
            rounded = round_and_deal_weight(w1_rows[k_pass, 1], f"w1_bf_{k_pass}1")
            w1_mx[k_pass, 1] = quantize(rounded[:], PASS, f"w1_{k_pass}1")
        v3 = gather_words(tab3, idx3, "v3")
        v2 = gather_words(tab2, idx2, "v2")
        turn_gains = keep.tile([P, SLICES], F32, name="turn_gains")
        for g in range(2):
            nc.scalar.activation(turn_gains[:, PACK * g : PACK * (g + 1)], gains[g][:], ACT.Copy, scale=TWO_PI)

        A_ROW = SLICES + 1
        work = keep.tile([P, A_ROW + SLICES, PICKS], F32, name="work")
        a_rows, b_rows, d_rows, whole, trig = {}, {}, {}, {}, {}

        def stage_bank(shape, name):
            return psum.tile(shape, F32, name=name, tag="stage", bufs=STAGE_BANKS)

        def chain_tile(shape, dtype, name, slot):
            return ring.tile(shape, dtype, name=name, tag=f"chain_{slot % CHAIN_SLOTS}", bufs=1)

        def multiply_a_d(s):
            g, t = divmod(s, PACK)
            cols = slice(P * t, P * (t + 1))
            a_rows[s] = ring.tile([P, S], F32, name=f"a_{s}", tag="a", bufs=ROW_TILES)
            d_rows[s] = chain_tile([P, S], F32, f"d_{s}", s)
            for half in range(S // BANK):
                m = slice(BANK * half, BANK * (half + 1))
                acc = stage_bank([P, BANK], f"a_acc_{s}_{half}")
                for k_pass in range(2):
                    codes, plane = w1_mx[k_pass, g]
                    nc.tensor.matmul_mx(
                        acc[:], lhsT=codes[:, cols].bitcast(FP8X4), lhsT_scale=plane[:, cols],
                        rhs=v_passes[k_pass][:, m].bitcast(FP8X4), rhs_scale=v_plane[4 * k_pass : P, m],
                        start=(k_pass == 0), stop=(k_pass == 1),
                    )
                nc.scalar.activation(a_rows[s][:, m], acc[:], ACT.Copy, scale=1.0 / TWO_PI)
            for half in range(S // BANK):
                m = slice(BANK * half, BANK * (half + 1))
                acc = stage_bank([P, BANK], f"d_acc_{s}_{half}")
                nc.tensor.matmul_mx(
                    acc[:], lhsT=w3_by_pass[g][:, cols].bitcast(FP8X4), lhsT_scale=w23_plane_by_pass[g][4:P, cols],
                    rhs=v3[:, m].bitcast(FP8X4), rhs_scale=v3_plane[:, m], start=True, stop=True,
                )
                nc.scalar.activation(d_rows[s][:, m], acc[:], ACT.Copy, scale=1.0 / TWO_PI, bias=0.25)

        def multiply_b(s):
            g, t = divmod(s, PACK)
            b_rows[s] = ring.tile([P, S], F32, name=f"b_{s}", tag="b", bufs=ROW_TILES)
            for half in range(S // BANK):
                m = slice(BANK * half, BANK * (half + 1))
                acc = stage_bank([P, BANK], f"b_acc_{s}_{half}")
                nc.tensor.matmul_mx(
                    acc[:], lhsT=w2_by_pass[g][:, 2 * P * t : 2 * P * (t + 1)].bitcast(FP4X4),
                    lhsT_scale=w23_plane_by_pass[g][:, P * t : P * (t + 1)],
                    rhs=v2[:, m].bitcast(FP8X4), rhs_scale=v2_plane[:, m], start=True, stop=True,
                )
                nc.scalar.activation(b_rows[s][:, m], acc[:], ACT.Copy, scale=gains[g][:, t : t + 1])

        def pick_angles(s):
            nc.vector.tensor_copy(work[:, A_ROW + s, :], a_rows[s][:].indirect(p1[:]))
            nc.vector.tensor_copy(work[:, s, :], d_rows[s][:].indirect(p3[:]))

        def picked_turns(s):
            return work[:, s : A_ROW + s + 1 : A_ROW, :]

        def round_turns(s):
            whole[s] = chain_tile([P, 2, PICKS], I32, f"whole_{s}", s - 1)
            if s + 1 < SLICES:
                nc.gpsimd.tensor_scalar(whole[s][:], picked_turns(s), 1.0, ROUNDER, ALU.mult, ALU.add)
            else:
                nc.scalar.activation(whole[s][:].bitcast(U32), picked_turns(s), ACT.Copy, bias=ROUNDER)

        def sines(s):
            trig[s] = chain_tile([P, 2, PICKS], F32, f"trig_{s}", s + 1)
            nc.vector.scalar_tensor_tensor(trig[s][:], whole[s][:], ROUNDER, picked_turns(s), ALU.subtract, ALU.subtract)
            nc.scalar.activation(trig[s][:], trig[s][:], ACT.Sin, scale=-TWO_PI)

        def terms(s):
            picked_a = work[:, A_ROW + s, :]
            nc.vector.scalar_tensor_tensor(picked_a, trig[s][:, 0, :], turn_gains[:, s : s + 1], picked_a, ALU.mult, ALU.mult)
            nc.vector.tensor_tensor(work[:, s + 1, :], b_rows[s][:].indirect(p2[:]), trig[s][:, 1, :], ALU.mult)

        identity = keep.tile([P, P], F32, name="identity")
        make_identity(nc, identity[:])
        z_turned = keep.tile([P, BLOCKS, 2, P, 2], BF16, name="z_turned")

        def add_turned(s):
            acc = psum.tile([P, BLOCKS, P], F32, name=f"z_sum_{s}", tag="turn", bufs=TURN_BANKS)
            for block in range(BLOCKS):
                js = slice(BLOCK * block, BLOCK * (block + 1))
                for row, opens in ((s + 1, True), (A_ROW + s, False)):
                    nc.tensor.matmul(
                        acc[:, block, :], lhsT=work[:, row, js], rhs=identity[:], is_transpose=True, start=opens, stop=not opens
                    )
            nc.scalar.copy(
                z_turned[:, :, :, 32 * s : 32 * (s + 1), :],
                acc[:].rearrange("j b (q u e) -> j b u q e", u=2, e=2),
            )

        def turn_back(z_pass):
            turned_pairs = z_turned[:].rearrange("j b u q e -> j b u (q e)").bitcast(F32)
            pairs = z_pass.bitcast(F32).rearrange("q (b j u) -> q b j u", j=BLOCK, u=2)
            for block in range(0, BLOCKS, 2):
                back = psum.tile([P, 2, 2, BLOCK], F32, name=f"z_back_{block}", tag="turn", bufs=TURN_BANKS)
                for b in range(2):
                    for u in range(2):
                        nc.tensor.transpose(back[:, b, u, :], turned_pairs[:, block + b, u, :], identity[:])
                nc.scalar.copy(pairs[:, block : block + 2], back[:].rearrange("q b u j -> q b j u"))

        y_acc = []

        def multiply_y(g, block, z_mx, first_column, width):
            codes, plane = z_mx
            z_cols = slice(first_column, first_column + BLOCK)
            abs_cols = slice(width + first_column, width + first_column + BLOCK)
            w5_codes, w5_plane = w5_mx[g]
            for t in range(PACK):
                cols = slice(P * t, P * (t + 1))
                w4_column = N * g + P * t
                nc.tensor.matmul_mx(
                    y_acc[block][:, t, :], lhsT=w4_dealt[:, 2 * w4_column : 2 * (w4_column + P)].bitcast(FP4X4),
                    lhsT_scale=w4_plane_dealt[:, w4_column : w4_column + P],
                    rhs=codes[:, z_cols].bitcast(FP8X4), rhs_scale=plane[:, z_cols],
                    start=(g == 0 and t == 0), stop=False,
                )
                nc.tensor.matmul_mx(
                    y_acc[block][:, t, :], lhsT=w5_codes[:, cols].bitcast(FP8X4), lhsT_scale=w5_plane[:, cols],
                    rhs=codes[:, abs_cols].bitcast(FP8X4), rhs_scale=plane[:, abs_cols],
                    start=False, stop=(g == 1 and t == PACK - 1),
                )

        w2_by_pass, w3_by_pass, w23_plane_by_pass = [w2_codes], [w3_codes], [w23_plane]
        multiply_a_d(0)
        multiply_a_d(1)
        w2_dealt = keep.tile([P, 2 * PASS], U8, name="w2_dealt", align_bytes=64)
        deal(w2_dealt[:].bitcast(U16), w2_codes[:, 2 * PASS : 2 * H].bitcast(U16), 8, 1)
        w3_dealt = keep.tile([P, PASS], I32, name="w3_dealt", align_bytes=64)
        deal(w3_dealt[:], w3_codes[:, PASS:H], 4, 1)
        w23_plane_dealt = keep.tile([P, PASS], U8, name="w23_plane_dealt", tag="tab2_plane", align_bytes=64)
        deal(w23_plane_dealt[:], w23_plane[:, PASS:H], 16, 1)
        w2_by_pass.append(w2_dealt)
        w3_by_pass.append(w3_dealt)
        w23_plane_by_pass.append(w23_plane_dealt)
        w5_mx = [quantize(round_and_deal_weight(w5_rows[g], f"w5_bf_{g}")[:], N, f"w5_{g}") for g in range(2)]

        PASS_0_TERMS_DONE = PACK + 1
        for i in range(SLICES + 2):
            if i < SLICES:
                pick_angles(i)
            if 1 <= i <= SLICES:
                sines(i - 1)
            if i == PACK:
                w4_dealt = keep.tile([P, 4 * N], U8, name="w4_dealt", tag="w1_10_codes", align_bytes=64)
                deal(w4_dealt[:].bitcast(U16), w4_codes[:].rearrange("p g c -> p (g c)").bitcast(U16), 8, 2)
                w4_plane_dealt = keep.tile([P, 2 * N], U8, name="w4_plane_dealt", tag="w1_00_codes", align_bytes=64)
                deal(w4_plane_dealt[:], w4_plane[:], 16, 2)
            if i + 2 < SLICES:
                multiply_a_d(i + 2)
            if i >= 2:
                terms(i - 2)
            if i < SLICES:
                round_turns(i)
                multiply_b(i)
            if 2 <= i <= PASS_0_TERMS_DONE:
                add_turned(i - 2)
            if i == PASS_0_TERMS_DONE:
                z_0 = large_tile([P, 2, PACK * PICKS], BF16, "z_0")
                turn_back(z_0[:, 0, :])
                nc.scalar.activation(z_0[:, 1, :], z_0[:, 0, :], ACT.Abs)
            if i == PASS_0_TERMS_DONE + 1:
                z_0_mx = quantize(z_0[:].rearrange("p a c -> p (a c)"), 2 * PICKS, "z_0")
            if i == SLICES - 1:
                for block in range(BLOCKS):
                    y_acc.append(stage_bank([P, PACK, BLOCK], f"y_acc_{block}"))
                    multiply_y(0, block, z_0_mx, BLOCK * block, PICKS)

        z_1 = []
        for block in range(BLOCKS + 1):
            if block < BLOCKS:
                z_1.append(ring.tile([P, 2, PACK * BLOCK], BF16, name=f"z_1_{block}", tag="z_1", bufs=BLOCKS, align_bytes=64))
                js = slice(BLOCK * block, BLOCK * (block + 1))
                nc.vector.tensor_tensor(
                    z_1[block][:, 0, :].rearrange("p (c i t) -> p c t i", i=2, t=PACK),
                    work[:, PACK + 1 : SLICES + 1, js].rearrange("p t (c i) -> p c t i", i=2),
                    work[:, A_ROW + PACK : A_ROW + SLICES, js].rearrange("p t (c i) -> p c t i", i=2),
                    ALU.add,
                )
                nc.scalar.activation(z_1[block][:, 1, :], z_1[block][:, 0, :], ACT.Abs)
            if block >= 1:
                z_1_mx = quantize(z_1[block - 1][:].rearrange("p a c -> p (a c)"), 2 * BLOCK, f"z_1_{block - 1}")
                multiply_y(1, block - 1, z_1_mx, 0, BLOCK)

        y_codes = keep.tile([P, PICKS], U32, name="y_codes", align_bytes=64)
        y_plane = keep.tile([P, PICKS], U8, name="y_plane", align_bytes=64)
        out_rows = out_0.rearrange("(p t) j -> p t j", t=PACK)
        out_words = out_1[0].rearrange("p j t -> p (j t)").bitcast(I32)
        for block in range(BLOCKS):
            js = slice(BLOCK * block, BLOCK * (block + 1))
            y = ring.tile([P, PACK, BLOCK], F32, name=f"y_{block}", tag="y", bufs=BLOCKS)
            nc.scalar.copy(y[:], y_acc[block][:])
            nc.sync.dma_start(out_rows[:, :, js], y[:])
            y_bf = ring.tile([P, PACK * BLOCK], BF16, name=f"y_bf_{block}", tag="y_bf", align_bytes=64)
            nc.vector.tensor_copy(
                y_bf[:].rearrange("p (c i t) -> p c t i", i=2, t=PACK),
                y[:].rearrange("p t (c i) -> p c t i", i=2),
            )
            nc.vector.quantize_mx(out=y_codes[:, js].bitcast(FP8X4), scales=y_plane[:, js], in_=y_bf[:])
            if block >= BLOCKS - 2:
                done = js if block == BLOCKS - 1 else slice(0, js.stop)
                nc.scalar.dma_start(out_words[:, done], y_codes[:, done].bitcast(I32))
        for quadrant in range(4):
            queue = nc.sync if quadrant % 2 == 0 else nc.scalar
            queue.dma_start(
                out_2[0, 4 * quadrant : 4 * quadrant + 4, :].bitcast(I32),
                y_plane[32 * quadrant : 32 * quadrant + 4, :].bitcast(I32),
            )
